import numpy as np
import ml_dtypes


def mxq(x, axis, fmt="e4m3"):
    dtype, down = {"e4m3": (ml_dtypes.float8_e4m3fn, 7), "e5m2": (ml_dtypes.float8_e5m2, 14)}[fmt]
    v = np.moveaxis(np.asarray(x, np.float32).astype(ml_dtypes.bfloat16).astype(np.float64), axis, -1)
    blocks = v.reshape(v.shape[:-1] + (-1, 32))
    amax = np.abs(blocks).max(-1, keepdims=True)
    byte = np.maximum(np.where(amax > 0, np.frexp(amax)[1] - 1 + 127, 0) - down, 1)
    scale = np.exp2(byte - 127.0)
    codes = (blocks / scale).astype(np.float32).astype(dtype).astype(np.float64)
    return np.moveaxis((codes * scale).reshape(v.shape), -1, axis)


WIDE = False


def mx_kscale(k):
    if not WIDE:
        return np.ones(k)
    levels = np.array([10, -10, 5, -5, 0])
    if k % 512:
        return np.exp2(np.random.permutation(np.resize(levels, k // 32))).repeat(32)
    a = np.empty((k // 512, 16))
    for p in range(k // 512):
        a[p, :8] = np.random.permutation(np.resize(levels, 8))
        for g in range(8):
            far = levels[np.abs(levels - a[p, g]) >= 10]
            a[p, g + 8] = far[np.random.randint(len(far))]
    return np.exp2(a.ravel()).repeat(32)


BF16 = ml_dtypes.bfloat16


def bf(x):
    return np.asarray(x, np.float32).astype(BF16)


def f64(x):
    return np.asarray(x).astype(np.float64)


E2M1 = np.array([0.0, 0.5, 1.0, 1.5, 2.0, 3.0, 4.0, 6.0, -0.0, -0.5, -1.0, -1.5, -2.0, -3.0, -4.0, -6.0])


def pack_weight(w, fmt):
    k, n = w.shape
    w = f64(bf(w)).reshape(k // 32, 32, n)
    amax = np.abs(w).max(1)
    if fmt == "e4m3":
        byte = np.frexp(amax)[1] - 1 + 127 - 7
    else:
        mant, ex = np.frexp(amax / 6.0)
        byte = np.where(mant > 0.5, ex, ex - 1) + 127
    byte = np.clip(np.where(amax > 0, byte, 1), 1, 254)
    scaled = (w * np.exp2(127.0 - byte)[:, None, :]).reshape(k, n).astype(np.float32)
    by_word = np.ascontiguousarray(scaled.reshape(k // 512, 128, 4, n).transpose(0, 1, 3, 2))
    if fmt == "e4m3":
        words = by_word.astype(ml_dtypes.float8_e4m3fn).view(np.uint8)
    else:
        c = by_word.astype(ml_dtypes.float4_e2m1fn).view(np.uint8) & 0xF
        words = c[..., 0::2] | (c[..., 1::2] << 4)
    return np.ascontiguousarray(words), np.ascontiguousarray(byte.astype(np.uint8).reshape(k // 512, 16, n))


def unpack_weight(words, scales, fmt):
    g, p, n, _ = words.shape
    if fmt == "e4m3":
        vals = np.ascontiguousarray(words).view(ml_dtypes.float8_e4m3fn).astype(np.float64)
    else:
        nib = np.empty((g, p, n, 4), np.uint8)
        nib[..., 0::2] = words & 0xF
        nib[..., 1::2] = words >> 4
        vals = E2M1[nib]
    vals = vals * np.repeat(np.exp2(scales.astype(np.float64) - 127.0), 8, axis=1)[..., None]
    return vals.transpose(0, 1, 3, 2).reshape(g * 512, n)
def pack4(w):
    words, scales = pack_weight(w, "e2m1")
    return words.reshape(words.shape[0], 128, -1), scales


def unpack4(words, scales):
    return unpack_weight(words.reshape(words.shape[0], 128, -1, 2), scales, "e2m1")


def planes(Y):
    n, m = Y.shape
    b = f64(bf(Y)).reshape(n // 32, 32, m)
    amax = np.abs(b).max(1)
    byte = np.clip(np.where(amax > 0, np.frexp(amax)[1] - 1 + 127 - 7, 1), 1, 254)
    codes = (b * np.exp2(127.0 - byte)[:, None, :]).reshape(n, m).astype(np.float32).astype(ml_dtypes.float8_e4m3fn).view(np.uint8)
    words = codes.reshape(n // 512, 128, 4, m).transpose(0, 1, 3, 2)
    return np.ascontiguousarray(words), np.ascontiguousarray(byte.astype(np.uint8).reshape(n // 512, 16, m))


M, K, F, D = 768, 1536, 2048, 1024
GELU_A, GELU_B = 0.7978845608028654, 0.044715


def gelu(u):
    return 0.5 * u * (1.0 + np.tanh(GELU_A * (u + GELU_B * u * u * u)))


def setup_inputs():
    s = mx_kscale(K)
    t = mx_kscale(F)
    xt = np.random.randn(K, M) * s[:, None]
    w1 = 1.5 * np.random.randn(K, F) / np.sqrt(K) / s[:, None]
    x_words, x_scales = pack_weight(xt, "e4m3")
    w1_words, w1_scales = pack4(w1)
    hidden_scale = bf((1.0 + 0.1 * np.random.randn(F)) * t)
    w2 = bf(1.5 * np.random.randn(F, D) / np.sqrt(F) / t[:, None])
    b2 = bf(0.3 * np.random.randn(D))
    dim_weight = bf(np.exp(0.8 * np.random.randn(D)))
    caption_weight = bf(np.exp(0.3 * np.random.randn(M)))
    return {"x_words": x_words, "x_scales": x_scales, "w1_words": w1_words, "w1_scales": w1_scales,
            "hidden_scale": hidden_scale, "w2": w2, "b2": b2,
            "dim_weight": dim_weight, "caption_weight": caption_weight}


def reference(x_words, x_scales, w1_words, w1_scales, hidden_scale, w2, b2, dim_weight, caption_weight):
    X = unpack_weight(x_words, x_scales, "e4m3").T
    W1 = unpack4(w1_words, w1_scales)
    U = X @ W1
    H = gelu(U) * f64(hidden_scale)[None, :]
    Z = mxq(H, 1, "e4m3") @ mxq(f64(w2), 0, "e4m3")
    y = (Z + f64(b2)[None, :]) * f64(dim_weight)[None, :] * f64(caption_weight)[:, None]
    words, scales = planes(y.T)
    return y, words, scales

@@ -1,0 +1,369 @@
+from contextlib import ExitStack
+
+import concourse.mybir as mybir
+from concourse.masks import make_identity
+
+M, K, F, D = 768, 1536, 2048, 1024
+FLOPS = 2 * M * K * F + 2 * M * F * D
+
+F32 = mybir.dt.float32
+BF16 = mybir.dt.bfloat16
+I32 = mybir.dt.int32
+U32 = mybir.dt.uint32
+U8 = mybir.dt.uint8
+FP8X4 = mybir.dt.float8_e4m3fn_x4
+FP4X4 = mybir.dt.float4_e2m1fn_x4
+ACT = mybir.ActivationFunctionType
+MULT = mybir.AluOpType.mult
+
+P = 128
+PACK = 4
+GROUP = P * PACK
+K_PASSES = K // GROUP
+F_GROUPS = F // GROUP
+D_GROUPS = D // GROUP
+BANKS = 8
+WIDE, NARROW = "wide", "narrow"
+CHUNK = {WIDE: (0, 512), NARROW: (512, 256)}
+
+
+def tile_caption_shared_embedding_h2_kernel(
+    tc, x_words, x_scales, w1_words, w1_scales, hidden_scale, w2, b2, dim_weight, caption_weight, out_0, out_1, out_2
+):
+    nc = tc.nc
+    with ExitStack() as ctx:
+        keep = ctx.enter_context(tc.tile_pool(name="keep", bufs=1))
+        work = ctx.enter_context(tc.tile_pool(name="work", bufs=3))
+        psum = ctx.enter_context(tc.psum_pool(name="psum", bufs=1))
+        ctx.enter_context(tc.manual_schedule())
+
+        banks_used = []
+
+        def next_bank(shape):
+            n = len(banks_used)
+            banks_used.append(n)
+            return psum.tile(shape, F32, name="bank_%d" % n, tag="bank%d" % (n % BANKS))
+
+        def kept(name, shape, dtype):
+            return keep.tile(shape, dtype, name=name, align_bytes=64)
+
+        x_codes = {c: kept("x_codes_" + c, [P, K_PASSES, CHUNK[c][1]], I32) for c in CHUNK}
+        x_plane = kept("x_plane", [P, K_PASSES, M], U8)
+        w1_raw = [kept("w1_raw%d" % g, [P, K_PASSES, 256], I32) for g in range(F_GROUPS)]
+        w1_plane_raw = kept("w1_plane_raw", [P, K_PASSES, F], U8)
+        w1_codes = [kept("w1_codes%d" % g, [P, PACK, K_PASSES, 2 * P], U8) for g in range(F_GROUPS)]
+        w1_plane = [kept("w1_plane%d" % g, [P, PACK, K_PASSES, P], U8) for g in range(F_GROUPS)]
+        w2_raw = [kept("w2_raw%d" % g, [P, PACK, D], BF16) for g in range(F_GROUPS)]
+        w2_codes = {(g, h): kept("w2_codes%d%d" % (g, h), [P, GROUP], U32) for g in range(F_GROUPS) for h in range(D_GROUPS)}
+        w2_plane = {(g, h): kept("w2_plane%d%d" % (g, h), [P, GROUP], U8) for g in range(F_GROUPS) for h in range(D_GROUPS)}
+        h_codes = {(c, g): kept("h_codes%s%d" % (c, g), [P, CHUNK[c][1]], U32) for c in CHUNK for g in range(F_GROUPS)}
+        h_plane = {(c, g): kept("h_plane%s%d" % (c, g), [P, CHUNK[c][1]], U8) for c in CHUNK for g in range(F_GROUPS)}
+        y_codes = {(c, h): kept("y_codes%s%d" % (c, h), [P, CHUNK[c][1]], U32) for c in CHUNK for h in range(D_GROUPS)}
+        y_plane = [kept("y_plane%d" % h, [P, M], U8) for h in range(D_GROUPS)]
+        raw_gain = kept("raw_gain", [P, GROUP], BF16)
+        raw_bias = kept("raw_bias", [P, GROUP], BF16)
+        raw_cap = kept("raw_cap", [P, GROUP], BF16)
+        rows = kept("rows", [P, GROUP], F32)
+        vec = kept("vec", [P, 3, PACK, PACK], F32)
+        bias = kept("bias", [P, D_GROUPS, PACK], F32)
+        cap_row = kept("cap_row", [P, M], BF16)
+        ident = kept("ident", [P, P], F32)
+        warm = kept("warm", [P, 1], F32)
+
+        def load_x(c):
+            m0, w = CHUNK[c]
+            src = x_words.rearrange("c p m t -> p c (m t)")[:, :, 4 * m0 : 4 * (m0 + w)]
+            nc.sync.dma_start(out=x_codes[c][:], in_=src.bitcast(I32))
+
+        def load_w1(g):
+            src = w1_words.rearrange("c p n -> p c n")[:, :, 1024 * g : 1024 * (g + 1)]
+            nc.sync.dma_start(out=w1_raw[g][:], in_=src.bitcast(I32))
+
+        def load_plane(plane, scales):
+            src = scales.rearrange("c q n -> q c n")
+            for quad in range(4):
+                nc.sync.dma_start(
+                    out=plane[32 * quad : 32 * quad + 4].bitcast(I32), in_=src[4 * quad : 4 * quad + 4].bitcast(I32)
+                )
+
+        def load_w2(g):
+            src = w2[GROUP * g : GROUP * (g + 1), :].rearrange("(q t r) n -> t q r n", t=PACK, r=8)
+            for t in range(PACK):
+                nc.sync.dma_start(out=w2_raw[g][:, t, :], in_=src[t])
+
+        nc.vector.memset(warm[:], 0.0)
+        nc.scalar.activation(out=warm[:], in_=warm[:], func=ACT.Gelu_apprx_tanh)
+        nc.vector.memset(w1_plane_raw[:].bitcast(I32), 0)
+        nc.vector.memset(x_plane[:].bitcast(I32), 0)
+        nc.vector.memset(rows[:], 0.0)
+        nc.gpsimd.dma_start(out=raw_gain[0:4, :], in_=hidden_scale.rearrange("(g f) -> g f", f=GROUP))
+        nc.gpsimd.dma_start(out=raw_bias[32:34, :], in_=b2.rearrange("(h d) -> h d", d=GROUP))
+        nc.gpsimd.dma_start(out=raw_bias[34:36, :], in_=dim_weight.rearrange("(h d) -> h d", d=GROUP))
+        nc.gpsimd.dma_start(out=raw_cap[64:66, 0:384], in_=caption_weight.rearrange("(a m) -> a m", a=2))
+        make_identity(nc, ident[:])
+
+        load_x(NARROW)
+        load_w1(0)
+        load_plane(w1_plane_raw, w1_scales)
+        load_plane(x_plane, x_scales)
+        load_w2(0)
+        load_x(WIDE)
+        load_w1(1)
+        load_w1(2)
+        load_w2(1)
+        load_w1(3)
+        load_w2(2)
+        load_w2(3)
+        nc.sync.dma_start(out=cap_row[:], in_=caption_weight.partition_broadcast(P))
+
+        def vectors():
+            nc.scalar.copy(
+                out=rows[0:4, :].rearrange("g (t q r) -> g t q r", t=PACK, r=8),
+                in_=raw_gain[0:4, :].rearrange("g (q t r) -> g t q r", t=PACK, r=8),
+            )
+            nc.scalar.copy(
+                out=rows[32:36, :].rearrange("g (t p) -> g t p", t=PACK),
+                in_=raw_bias[32:36, :].rearrange("g (p t) -> g t p", t=PACK),
+            )
+            nc.scalar.copy(out=rows[64:66, 0:384], in_=raw_cap[64:66, 0:384])
+
+        def turn_vectors():
+            bank = next_bank([P, PACK, P])
+            for t in range(PACK):
+                nc.tensor.transpose(bank[:, t, :], rows[:, P * t : P * (t + 1)], ident[:])
+            nc.scalar.copy(
+                out=vec[:], in_=bank[:].rearrange("p t (a b) -> p a b t", b=32)[:, 0:3, 0:PACK, :]
+            )
+
+        def bias_product():
+            nc.vector.tensor_tensor(out=bias[:], in0=vec[:, 1, 0:2, :], in1=vec[:, 1, 2:4, :], op=MULT)
+
+        def order_w1(g):
+            nc.vector.tensor_copy(
+                out=w1_codes[g][:].bitcast(I32).rearrange("p t c (q w) -> p t (c q) w", w=4),
+                in_=w1_raw[g][:].rearrange("p c (q t w) -> p t (c q) w", t=PACK, w=4),
+            )
+            src = w1_plane_raw[:].bitcast(I32)[:, :, P * g : P * (g + 1)]
+            nc.vector.tensor_copy(
+                out=w1_plane[g][:].bitcast(I32).rearrange("p t c (q w) -> p t c q w", w=2),
+                in_=src.rearrange("p c (q t w) -> p t c q w", t=PACK, w=2),
+            )
+
+        gelu_of = {}
+        h_bf = {}
+
+        def hidden(c, g):
+            m0, w = CHUNK[c]
+
+            def passes(out, t, lo, n):
+                for k in range(K_PASSES):
+                    nc.tensor.matmul_mx(
+                        out=out,
+                        lhsT=w1_codes[g][:, t, k, :].bitcast(FP4X4),
+                        lhsT_scale=w1_plane[g][:, t, k, :],
+                        rhs=x_codes[c][:, k, lo : lo + n].bitcast(FP8X4),
+                        rhs_scale=x_plane[:, k, m0 + lo : m0 + lo + n],
+                        start=(k == 0),
+                        stop=(k == K_PASSES - 1),
+                    )
+
+            if c == WIDE:
+                act = work.tile([P, PACK, w], F32, name="gelu_%s%d" % (c, g), tag="f32")
+                for t in range(PACK):
+                    bank = next_bank([P, w])
+                    passes(bank[:], t, 0, w)
+                    nc.scalar.activation(out=act[:, t, :], in_=bank[:], func=ACT.Gelu_apprx_tanh)
+            else:
+                act = work.tile([P, w, PACK], F32, name="gelu_%s%d" % (c, g), tag="f32")
+                for lo in range(0, w, P):
+                    bank = next_bank([P, PACK, P])
+                    for t in range(PACK):
+                        passes(bank[:, t, :], t, lo, P)
+                    nc.scalar.activation(
+                        out=act[:, lo : lo + P, :], in_=bank[:].rearrange("p t m -> p m t"), func=ACT.Gelu_apprx_tanh
+                    )
+            gelu_of[c, g] = act
+
+        def scale_hidden(c, g):
+            w = CHUNK[c][1]
+            hb = work.tile([P, w, PACK], BF16, name="h_bf_%s%d" % (c, g), tag="bf", align_bytes=64)
+            gain = vec[:, 0, g, :]
+            if c == WIDE:
+                nc.vector.tensor_tensor(
+                    out=hb[:].rearrange("p (n i) t -> p n t i", i=2),
+                    in0=gelu_of[c, g][:].rearrange("p t (n i) -> p n t i", i=2),
+                    in1=gain.unsqueeze(1).unsqueeze(3).broadcast_to([P, w // 2, PACK, 2]),
+                    op=MULT,
+                )
+            else:
+                nc.vector.tensor_tensor(
+                    out=hb[:], in0=gelu_of[c, g][:], in1=gain.unsqueeze(1).broadcast_to([P, w, PACK]), op=MULT
+                )
+            h_bf[c, g] = hb
+
+        def quantize(codes, plane, values):
+            nc.vector.quantize_mx(
+                out=codes.bitcast(FP8X4), scales=plane, in_=values[:].rearrange("p n t -> p (n t)")
+            )
+
+        def quantize_hidden(c, g):
+            quantize(h_codes[c, g][:], h_plane[c, g][:], h_bf[c, g])
+
+        w2_bf = {}
+
+        def group_w2(g, h, on_scalar):
+            wb = work.tile([P, GROUP, PACK], BF16, name="w2_bf%d%d" % (g, h), tag="w2bf", align_bytes=64)
+            out = wb[:].rearrange("p (t m) j -> p m j t", t=PACK)
+            in_ = w2_raw[g][:, :, GROUP * h : GROUP * (h + 1)].rearrange("p j (m t) -> p m j t", t=PACK)
+            if on_scalar:
+                nc.scalar.copy(out=out, in_=in_)
+            else:
+                nc.vector.tensor_copy(out=out, in_=in_)
+            w2_bf[g, h] = wb
+
+        def quantize_w2(g, h):
+            quantize(w2_codes[g, h][:], w2_plane[g, h][:], w2_bf[g, h])
+
+        affine_of = {}
+        y_bf = {}
+
+        def project(c, h):
+            w = CHUNK[c][1]
+            per_bank = 512 // w
+            aff = work.tile([P, PACK, w], F32, name="aff_%s%d" % (c, h), tag="f32")
+            for t0 in range(0, PACK, per_bank):
+                bank = next_bank([P, per_bank, w])
+                for s in range(per_bank):
+                    t = t0 + s
+                    for g in range(F_GROUPS):
+                        nc.tensor.matmul_mx(
+                            out=bank[:, s, :],
+                            lhsT=w2_codes[g, h][:, P * t : P * (t + 1)].bitcast(FP8X4),
+                            lhsT_scale=w2_plane[g, h][:, P * t : P * (t + 1)],
+                            rhs=h_codes[c, g][:].bitcast(FP8X4),
+                            rhs_scale=h_plane[c, g][:],
+                            start=(g == 0),
+                            stop=(g == F_GROUPS - 1),
+                        )
+                for s in range(per_bank):
+                    t = t0 + s
+                    nc.scalar.activation(
+                        out=aff[:, t, :],
+                        in_=bank[:, s, :],
+                        func=ACT.Identity,
+                        scale=vec[:, 1, 2 + h, t : t + 1],
+                        bias=bias[:, h, t : t + 1],
+                    )
+            affine_of[c, h] = aff
+
+        def rows_out(c, h):
+            m0, w = CHUNK[c]
+            turned = []
+            for lo in range(0, w, P):
+                bank = next_bank([P, PACK, P])
+                for t in range(PACK):
+                    nc.tensor.transpose(bank[:, t, :], affine_of[c, h][:, t, lo : lo + P], ident[:])
+                turned.append(bank)
+            for i, bank in enumerate(turned):
+                mt = m0 // P + i
+                y = work.tile([P, P, PACK], F32, name="y_%d%d" % (mt, h), tag="y", bufs=4)
+                nc.scalar.activation(
+                    out=y[:],
+                    in_=bank[:].rearrange("m t p -> m p t"),
+                    func=ACT.Copy,
+                    scale=vec[:, 2, mt // 3, mt % 3 : mt % 3 + 1],
+                )
+                nc.sync.dma_start(
+                    out=out_0[P * mt : P * (mt + 1), GROUP * h : GROUP * (h + 1)], in_=y[:].rearrange("m p t -> m (p t)")
+                )
+
+        def scale_y(c, h):
+            m0, w = CHUNK[c]
+            yb = work.tile([P, w, PACK], BF16, name="y_bf_%s%d" % (c, h), tag="bf", align_bytes=64)
+            cap = cap_row[:, m0 : m0 + w].rearrange("p (n i) -> p n i", i=2)
+            nc.vector.tensor_tensor(
+                out=yb[:].rearrange("p (n i) t -> p n t i", i=2),
+                in0=affine_of[c, h][:].rearrange("p t (n i) -> p n t i", i=2),
+                in1=cap.unsqueeze(2).broadcast_to([P, w // 2, PACK, 2]),
+                op=MULT,
+            )
+            y_bf[c, h] = yb
+
+        def quantize_y(c, h):
+            m0, w = CHUNK[c]
+            quantize(y_codes[c, h][:], y_plane[h][:, m0 : m0 + w], y_bf[c, h])
+            dst = out_1[h].rearrange("p m t -> p (m t)")[:, 4 * m0 : 4 * (m0 + w)]
+            nc.sync.dma_start(out=dst.bitcast(I32), in_=y_codes[c, h][:].bitcast(I32))
+
+        def store_plane(h):
+            for quad in range(4):
+                nc.sync.dma_start(
+                    out=out_2[h, 4 * quad : 4 * quad + 4, :].bitcast(I32),
+                    in_=y_plane[h][32 * quad : 32 * quad + 4, :].bitcast(I32),
+                )
+
+        vectors()
+        order_w1(0)
+        hidden(NARROW, 0)
+        turn_vectors()
+        group_w2(0, 0, False)
+        group_w2(0, 1, False)
+        quantize_w2(0, 0)
+        order_w1(1)
+        quantize_w2(0, 1)
+        hidden(WIDE, 0)
+        scale_hidden(NARROW, 0)
+        bias_product()
+        order_w1(2)
+        quantize_hidden(NARROW, 0)
+        group_w2(1, 0, True)
+        hidden(WIDE, 1)
+        scale_hidden(WIDE, 0)
+        order_w1(3)
+        quantize_hidden(WIDE, 0)
+        group_w2(1, 1, False)
+        quantize_w2(1, 0)
+        group_w2(2, 0, True)
+        hidden(WIDE, 2)
+        scale_hidden(WIDE, 1)
+        quantize_w2(1, 1)
+        quantize_hidden(WIDE, 1)
+        quantize_w2(2, 0)
+        hidden(WIDE, 3)
+        scale_hidden(WIDE, 2)
+        group_w2(3, 0, True)
+        quantize_hidden(WIDE, 2)
+        hidden(NARROW, 1)
+        scale_hidden(WIDE, 3)
+        quantize_w2(3, 0)
+        quantize_hidden(WIDE, 3)
+        hidden(NARROW, 2)
+        hidden(NARROW, 3)
+        scale_hidden(NARROW, 1)
+        scale_hidden(NARROW, 2)
+        quantize_hidden(NARROW, 1)
+        group_w2(2, 1, True)
+        project(WIDE, 0)
+        scale_hidden(NARROW, 3)
+        quantize_hidden(NARROW, 2)
+        group_w2(3, 1, False)
+        quantize_hidden(NARROW, 3)
+        project(NARROW, 0)
+        quantize_w2(2, 1)
+        quantize_w2(3, 1)
+        rows_out(WIDE, 0)
+        scale_y(WIDE, 0)
+        project(WIDE, 1)
+        rows_out(NARROW, 0)
+        scale_y(NARROW, 0)
+        quantize_y(WIDE, 0)
+        quantize_y(NARROW, 0)
+        store_plane(0)
+        scale_y(WIDE, 1)
+        rows_out(WIDE, 1)
+        project(NARROW, 1)
+        quantize_y(WIDE, 1)
+        scale_y(NARROW, 1)
+        rows_out(NARROW, 1)
+        quantize_y(NARROW, 1)
+        store_plane(1)

@@ -15,6 +15,7 @@ FP8X4 = mybir.dt.float8_e4m3fn_x4
 FP4X4 = mybir.dt.float4_e2m1fn_x4
 ACT = mybir.ActivationFunctionType
 MULT = mybir.AluOpType.mult
+ADD = mybir.AluOpType.add
 
 P = 128
 PACK = 4
@@ -39,10 +40,10 @@ def tile_caption_shared_embedding_h2_kernel(
 
         banks_used = []
 
-        def next_bank(shape):
+        def next_bank(shape, dtype=F32):
             n = len(banks_used)
             banks_used.append(n)
-            return psum.tile(shape, F32, name="bank_%d" % n, tag="bank%d" % (n % BANKS))
+            return psum.tile(shape, dtype, name="bank_%d" % n, tag="bank%d" % (n % BANKS))
 
         def kept(name, shape, dtype):
             return keep.tile(shape, dtype, name=name, align_bytes=64)
@@ -50,7 +51,8 @@ def tile_caption_shared_embedding_h2_kernel(
         x_codes = {c: kept("x_codes_" + c, [P, K_PASSES, CHUNK[c][1]], I32) for c in CHUNK}
         x_plane = kept("x_plane", [P, K_PASSES, M], U8)
         w1_raw = [kept("w1_raw%d" % g, [P, K_PASSES, 256], I32) for g in range(F_GROUPS)]
-        w1_plane_raw = kept("w1_plane_raw", [P, K_PASSES, F], U8)
+        w1_plane_first = kept("w1_plane_first", [P, K_PASSES, GROUP], U8)
+        w1_plane_rest = kept("w1_plane_rest", [P, K_PASSES, F - GROUP], U8)
         w1_codes = [kept("w1_codes%d" % g, [P, PACK, K_PASSES, 2 * P], U8) for g in range(F_GROUPS)]
         w1_plane = [kept("w1_plane%d" % g, [P, PACK, K_PASSES, P], U8) for g in range(F_GROUPS)]
         w2_raw = [kept("w2_raw%d" % g, [P, PACK, D], BF16) for g in range(F_GROUPS)]
@@ -60,14 +62,17 @@ def tile_caption_shared_embedding_h2_kernel(
         h_plane = {(c, g): kept("h_plane%s%d" % (c, g), [P, CHUNK[c][1]], U8) for c in CHUNK for g in range(F_GROUPS)}
         y_codes = {(c, h): kept("y_codes%s%d" % (c, h), [P, CHUNK[c][1]], U32) for c in CHUNK for h in range(D_GROUPS)}
         y_plane = [kept("y_plane%d" % h, [P, M], U8) for h in range(D_GROUPS)]
-        raw_gain = kept("raw_gain", [P, GROUP], BF16)
-        raw_bias = kept("raw_bias", [P, GROUP], BF16)
-        raw_cap = kept("raw_cap", [P, GROUP], BF16)
-        rows = kept("rows", [P, GROUP], F32)
-        vec = kept("vec", [P, 3, PACK, PACK], F32)
+        gain_raw = kept("gain_raw", [F_GROUPS, GROUP], BF16)
+        gain_rows = kept("gain_rows", [P, GROUP], F32)
+        gain = kept("gain", [P, F_GROUPS, PACK], F32)
+        b2_col = kept("b2_col", [P, D_GROUPS, PACK], BF16)
+        dim_col = kept("dim_col", [P, D_GROUPS, PACK], BF16)
+        dim_f32 = kept("dim_f32", [P, D_GROUPS, PACK], F32)
         bias = kept("bias", [P, D_GROUPS, PACK], F32)
         cap_row = kept("cap_row", [P, M], BF16)
+        cap_col = kept("cap_col", [P, M // P], F32)
         ident = kept("ident", [P, P], F32)
+        ident_bf = kept("ident_bf", [P, P], BF16)
         warm = kept("warm", [P, 1], F32)
 
         def load_x(c):
@@ -91,59 +96,78 @@ def tile_caption_shared_embedding_h2_kernel(
             for t in range(PACK):
                 nc.sync.dma_start(out=w2_raw[g][:, t, :], in_=src[t])
 
+        def load_gain():
+            nc.sync.dma_start(out=gain_raw[:], in_=hidden_scale.rearrange("(g f) -> g f", f=GROUP))
+
+        def turn_gain():
+            nc.scalar.copy(
+                out=gain_rows[0:F_GROUPS, :].rearrange("g (t q r) -> g t q r", t=PACK, r=8),
+                in_=gain_raw[:].rearrange("g (q t r) -> g t q r", t=PACK, r=8),
+            )
+            bank = next_bank([P, PACK, P])
+            for t in range(PACK):
+                nc.tensor.transpose(bank[:, t, :], gain_rows[:, P * t : P * (t + 1)], ident[:])
+            nc.scalar.copy(out=gain[:], in_=bank[:, :, 0:F_GROUPS].rearrange("p t g -> p g t"))
+
+        def load_late_vectors():
+            nc.sync.dma_start(out=b2_col[:], in_=b2.rearrange("(h p t) -> p h t", p=P, t=PACK))
+            nc.sync.dma_start(out=dim_col[:], in_=dim_weight.rearrange("(h p t) -> p h t", p=P, t=PACK))
+            nc.sync.dma_start(out=cap_row[:], in_=caption_weight.partition_broadcast(P))
+
         nc.vector.memset(warm[:], 0.0)
         nc.scalar.activation(out=warm[:], in_=warm[:], func=ACT.Gelu_apprx_tanh)
-        nc.vector.memset(w1_plane_raw[:].bitcast(I32), 0)
+        nc.vector.memset(w1_plane_first[:].bitcast(I32), 0)
         nc.vector.memset(x_plane[:].bitcast(I32), 0)
-        nc.vector.memset(rows[:], 0.0)
-        nc.gpsimd.dma_start(out=raw_gain[0:4, :], in_=hidden_scale.rearrange("(g f) -> g f", f=GROUP))
-        nc.gpsimd.dma_start(out=raw_bias[32:34, :], in_=b2.rearrange("(h d) -> h d", d=GROUP))
-        nc.gpsimd.dma_start(out=raw_bias[34:36, :], in_=dim_weight.rearrange("(h d) -> h d", d=GROUP))
-        nc.gpsimd.dma_start(out=raw_cap[64:66, 0:384], in_=caption_weight.rearrange("(a m) -> a m", a=2))
-        make_identity(nc, ident[:])
+        nc.vector.memset(ident[:], 0.0)
+        make_identity(nc, ident[:], nomemset=True)
+        nc.vector.memset(gain_rows[:], 0.0)
+        nc.vector.memset(w1_plane_rest[:].bitcast(I32), 0)
 
+        load_gain()
         load_x(NARROW)
         load_w1(0)
-        load_plane(w1_plane_raw, w1_scales)
+        load_plane(w1_plane_first, w1_scales[:, :, :GROUP])
         load_plane(x_plane, x_scales)
         load_w2(0)
         load_x(WIDE)
+        load_plane(w1_plane_rest, w1_scales[:, :, GROUP:])
         load_w1(1)
         load_w1(2)
         load_w2(1)
         load_w1(3)
         load_w2(2)
         load_w2(3)
-        nc.sync.dma_start(out=cap_row[:], in_=caption_weight.partition_broadcast(P))
+        load_late_vectors()
+        turn_gain()
 
-        def vectors():
-            nc.scalar.copy(
-                out=rows[0:4, :].rearrange("g (t q r) -> g t q r", t=PACK, r=8),
-                in_=raw_gain[0:4, :].rearrange("g (q t r) -> g t q r", t=PACK, r=8),
-            )
-            nc.scalar.copy(
-                out=rows[32:36, :].rearrange("g (t p) -> g t p", t=PACK),
-                in_=raw_bias[32:36, :].rearrange("g (p t) -> g t p", t=PACK),
-            )
-            nc.scalar.copy(out=rows[64:66, 0:384], in_=raw_cap[64:66, 0:384])
+        def turn_caption_weight():
+            bank = next_bank([P, M // P, P], BF16)
+            for mt in range(M // P):
+                nc.tensor.transpose(bank[:, mt, :], cap_row[:, P * mt : P * (mt + 1)], ident_bf[:])
+            return bank
 
-        def turn_vectors():
-            bank = next_bank([P, PACK, P])
-            for t in range(PACK):
-                nc.tensor.transpose(bank[:, t, :], rows[:, P * t : P * (t + 1)], ident[:])
-            nc.scalar.copy(
-                out=vec[:], in_=bank[:].rearrange("p t (a b) -> p a b t", b=32)[:, 0:3, 0:PACK, :]
-            )
+        def caption_column(bank, on_scalar):
+            if on_scalar:
+                nc.scalar.copy(out=cap_col[:], in_=bank[:, :, 0])
+            else:
+                nc.vector.tensor_copy(out=cap_col[:], in_=bank[:, :, 0])
 
         def bias_product():
-            nc.vector.tensor_tensor(out=bias[:], in0=vec[:, 1, 0:2, :], in1=vec[:, 1, 2:4, :], op=MULT)
+            nc.vector.tensor_copy(out=ident_bf[:], in_=ident[:])
+            nc.vector.tensor_copy(out=dim_f32[:], in_=dim_col[:])
+            nc.vector.tensor_tensor(out=bias[:], in0=b2_col[:], in1=dim_col[:], op=MULT)
 
-        def order_w1(g):
+        def order_w1_codes(g):
             nc.vector.tensor_copy(
                 out=w1_codes[g][:].bitcast(I32).rearrange("p t c (q w) -> p t (c q) w", w=4),
                 in_=w1_raw[g][:].rearrange("p c (q t w) -> p t (c q) w", t=PACK, w=4),
             )
-            src = w1_plane_raw[:].bitcast(I32)[:, :, P * g : P * (g + 1)]
+
+        def order_w1_plane(g):
+            if g == 0:
+                src = w1_plane_first[:].bitcast(I32)
+            else:
+                src = w1_plane_rest[:].bitcast(I32)[:, :, P * (g - 1) : P * g]
             nc.vector.tensor_copy(
                 out=w1_plane[g][:].bitcast(I32).rearrange("p t c (q w) -> p t c q w", w=2),
                 in_=src.rearrange("p c (q t w) -> p t c q w", t=PACK, w=2),
@@ -152,7 +176,9 @@ def tile_caption_shared_embedding_h2_kernel(
         gelu_of = {}
         h_bf = {}
 
-        def hidden(c, g):
+        bank_of = {}
+
+        def hidden_matmul(c, g, u):
             m0, w = CHUNK[c]
 
             def passes(out, t, lo, n):
@@ -168,36 +194,42 @@ def tile_caption_shared_embedding_h2_kernel(
                     )
 
             if c == WIDE:
-                act = work.tile([P, PACK, w], F32, name="gelu_%s%d" % (c, g), tag="f32")
-                for t in range(PACK):
-                    bank = next_bank([P, w])
-                    passes(bank[:], t, 0, w)
-                    nc.scalar.activation(out=act[:, t, :], in_=bank[:], func=ACT.Gelu_apprx_tanh)
+                bank = next_bank([P, w])
+                passes(bank[:], u, 0, w)
             else:
-                act = work.tile([P, w, PACK], F32, name="gelu_%s%d" % (c, g), tag="f32")
-                for lo in range(0, w, P):
-                    bank = next_bank([P, PACK, P])
-                    for t in range(PACK):
-                        passes(bank[:, t, :], t, lo, P)
-                    nc.scalar.activation(
-                        out=act[:, lo : lo + P, :], in_=bank[:].rearrange("p t m -> p m t"), func=ACT.Gelu_apprx_tanh
-                    )
-            gelu_of[c, g] = act
+                bank = next_bank([P, PACK, P])
+                for t in range(PACK):
+                    passes(bank[:, t, :], t, P * u, P)
+            bank_of["hidden", c, g, u] = bank
+
+        def gelu(c, g, u):
+            w = CHUNK[c][1]
+            bank = bank_of["hidden", c, g, u]
+            if (c, g) not in gelu_of:
+                shape = [P, PACK, w] if c == WIDE else [P, w, PACK]
+                gelu_of[c, g] = work.tile(shape, F32, name="gelu_%s%d" % (c, g), tag="f32", bufs=5)
+            act = gelu_of[c, g]
+            if c == WIDE:
+                nc.scalar.activation(out=act[:, u, :], in_=bank[:], func=ACT.Gelu_apprx_tanh)
+            else:
+                nc.scalar.activation(
+                    out=act[:, P * u : P * (u + 1), :], in_=bank[:].rearrange("p t m -> p m t"), func=ACT.Gelu_apprx_tanh
+                )
 
         def scale_hidden(c, g):
             w = CHUNK[c][1]
-            hb = work.tile([P, w, PACK], BF16, name="h_bf_%s%d" % (c, g), tag="bf", align_bytes=64)
-            gain = vec[:, 0, g, :]
+            hb = work.tile([P, w, PACK], BF16, name="h_bf_%s%d" % (c, g), tag="bf", bufs=4, align_bytes=64)
+            factor = gain[:, g, :]
             if c == WIDE:
                 nc.vector.tensor_tensor(
                     out=hb[:].rearrange("p (n i) t -> p n t i", i=2),
                     in0=gelu_of[c, g][:].rearrange("p t (n i) -> p n t i", i=2),
-                    in1=gain.unsqueeze(1).unsqueeze(3).broadcast_to([P, w // 2, PACK, 2]),
+                    in1=factor.unsqueeze(1).unsqueeze(3).broadcast_to([P, w // 2, PACK, 2]),
                     op=MULT,
                 )
             else:
                 nc.vector.tensor_tensor(
-                    out=hb[:], in0=gelu_of[c, g][:], in1=gain.unsqueeze(1).broadcast_to([P, w, PACK]), op=MULT
+                    out=hb[:], in0=gelu_of[c, g][:], in1=factor.unsqueeze(1).broadcast_to([P, w, PACK]), op=MULT
                 )
             h_bf[c, g] = hb
 
@@ -212,9 +244,9 @@ def tile_caption_shared_embedding_h2_kernel(
         w2_bf = {}
 
         def group_w2(g, h, on_scalar):
-            wb = work.tile([P, GROUP, PACK], BF16, name="w2_bf%d%d" % (g, h), tag="w2bf", align_bytes=64)
-            out = wb[:].rearrange("p (t m) j -> p m j t", t=PACK)
-            in_ = w2_raw[g][:, :, GROUP * h : GROUP * (h + 1)].rearrange("p j (m t) -> p m j t", t=PACK)
+            wb = work.tile([P, GROUP, PACK], BF16, name="w2_bf%d%d" % (g, h), tag="w2bf", bufs=6, align_bytes=64)
+            out = wb[:].rearrange("p (t m i) j -> p t m j i", t=PACK, i=2)
+            in_ = w2_raw[g][:, :, GROUP * h : GROUP * (h + 1)].rearrange("p j (m i t) -> p t m j i", t=PACK, i=2)
             if on_scalar:
                 nc.scalar.copy(out=out, in_=in_)
             else:
@@ -227,59 +259,63 @@ def tile_caption_shared_embedding_h2_kernel(
         affine_of = {}
         y_bf = {}
 
-        def project(c, h):
+        def project(c, h, u):
             w = CHUNK[c][1]
             per_bank = 512 // w
-            aff = work.tile([P, PACK, w], F32, name="aff_%s%d" % (c, h), tag="f32")
-            for t0 in range(0, PACK, per_bank):
-                bank = next_bank([P, per_bank, w])
-                for s in range(per_bank):
-                    t = t0 + s
-                    for g in range(F_GROUPS):
-                        nc.tensor.matmul_mx(
-                            out=bank[:, s, :],
-                            lhsT=w2_codes[g, h][:, P * t : P * (t + 1)].bitcast(FP8X4),
-                            lhsT_scale=w2_plane[g, h][:, P * t : P * (t + 1)],
-                            rhs=h_codes[c, g][:].bitcast(FP8X4),
-                            rhs_scale=h_plane[c, g][:],
-                            start=(g == 0),
-                            stop=(g == F_GROUPS - 1),
-                        )
-                for s in range(per_bank):
-                    t = t0 + s
-                    nc.scalar.activation(
-                        out=aff[:, t, :],
-                        in_=bank[:, s, :],
-                        func=ACT.Identity,
-                        scale=vec[:, 1, 2 + h, t : t + 1],
-                        bias=bias[:, h, t : t + 1],
+            bank = next_bank([P, per_bank, w])
+            for s in range(per_bank):
+                t = per_bank * u + s
+                for g in range(F_GROUPS):
+                    nc.tensor.matmul_mx(
+                        out=bank[:, s, :],
+                        lhsT=w2_codes[g, h][:, P * t : P * (t + 1)].bitcast(FP8X4),
+                        lhsT_scale=w2_plane[g, h][:, P * t : P * (t + 1)],
+                        rhs=h_codes[c, g][:].bitcast(FP8X4),
+                        rhs_scale=h_plane[c, g][:],
+                        start=(g == 0),
+                        stop=(g == F_GROUPS - 1),
                     )
-            affine_of[c, h] = aff
+            bank_of["project", c, h, u] = bank
 
-        def rows_out(c, h):
-            m0, w = CHUNK[c]
-            turned = []
-            for lo in range(0, w, P):
-                bank = next_bank([P, PACK, P])
-                for t in range(PACK):
-                    nc.tensor.transpose(bank[:, t, :], affine_of[c, h][:, t, lo : lo + P], ident[:])
-                turned.append(bank)
-            for i, bank in enumerate(turned):
-                mt = m0 // P + i
-                y = work.tile([P, P, PACK], F32, name="y_%d%d" % (mt, h), tag="y", bufs=4)
-                nc.scalar.activation(
-                    out=y[:],
-                    in_=bank[:].rearrange("m t p -> m p t"),
-                    func=ACT.Copy,
-                    scale=vec[:, 2, mt // 3, mt % 3 : mt % 3 + 1],
-                )
-                nc.sync.dma_start(
-                    out=out_0[P * mt : P * (mt + 1), GROUP * h : GROUP * (h + 1)], in_=y[:].rearrange("m p t -> m (p t)")
-                )
+        def affine(c, h, u, on_scalar):
+            w = CHUNK[c][1]
+            per_bank = 512 // w
+            bank = bank_of["project", c, h, u]
+            if (c, h) not in affine_of:
+                affine_of[c, h] = work.tile([P, PACK, w], F32, name="aff_%s%d" % (c, h), tag="f32", bufs=5)
+            for s in range(per_bank):
+                t = per_bank * u + s
+                scale = dim_f32[:, h, t : t + 1]
+                shift = bias[:, h, t : t + 1]
+                out = affine_of[c, h][:, t, :]
+                if on_scalar:
+                    nc.scalar.activation(out=out, in_=bank[:, s, :], func=ACT.Identity, scale=scale, bias=shift)
+                else:
+                    nc.vector.tensor_scalar(out=out, in0=bank[:, s, :], scalar1=scale, scalar2=shift, op0=MULT, op1=ADD)
+
+        def turn(mt, h):
+            c = WIDE if P * mt < CHUNK[NARROW][0] else NARROW
+            lo = P * mt - CHUNK[c][0]
+            bank = next_bank([P, PACK, P])
+            for t in range(PACK):
+                nc.tensor.transpose(bank[:, t, :], affine_of[c, h][:, t, lo : lo + P], ident[:])
+            bank_of["turn", mt, h] = bank
+
+        def rows_out(mt, h, on_scalar):
+            y = work.tile([P, P, PACK], F32, name="y_%d%d" % (mt, h), tag="y", bufs=6)
+            cap = cap_col[:, mt : mt + 1]
+            src = bank_of["turn", mt, h][:].rearrange("m t p -> m p t")
+            if on_scalar:
+                nc.scalar.activation(out=y[:], in_=src, func=ACT.Copy, scale=cap)
+            else:
+                nc.vector.tensor_scalar(out=y[:], in0=src, scalar1=cap, scalar2=None, op0=MULT)
+            nc.sync.dma_start(
+                out=out_0[P * mt : P * (mt + 1), GROUP * h : GROUP * (h + 1)], in_=y[:].rearrange("m p t -> m (p t)")
+            )
 
         def scale_y(c, h):
             m0, w = CHUNK[c]
-            yb = work.tile([P, w, PACK], BF16, name="y_bf_%s%d" % (c, h), tag="bf", align_bytes=64)
+            yb = work.tile([P, w, PACK], BF16, name="y_bf_%s%d" % (c, h), tag="bf", bufs=4, align_bytes=64)
             cap = cap_row[:, m0 : m0 + w].rearrange("p (n i) -> p n i", i=2)
             nc.vector.tensor_tensor(
                 out=yb[:].rearrange("p (n i) t -> p n t i", i=2),
@@ -302,68 +338,152 @@ def tile_caption_shared_embedding_h2_kernel(
                     in_=y_plane[h][32 * quad : 32 * quad + 4, :].bitcast(I32),
                 )
 
-        vectors()
-        order_w1(0)
-        hidden(NARROW, 0)
-        turn_vectors()
+        order_w1_codes(0)
+        order_w1_plane(0)
+        hidden_matmul(NARROW, 0, 0)
+        hidden_matmul(NARROW, 0, 1)
+        group_w2(0, 1, True)
+        gelu(NARROW, 0, 0)
+        gelu(NARROW, 0, 1)
         group_w2(0, 0, False)
-        group_w2(0, 1, False)
-        quantize_w2(0, 0)
-        order_w1(1)
+        hidden_matmul(WIDE, 0, 0)
+        hidden_matmul(WIDE, 0, 1)
+        hidden_matmul(WIDE, 0, 2)
+        hidden_matmul(WIDE, 0, 3)
+        gelu(WIDE, 0, 0)
+        gelu(WIDE, 0, 1)
+        gelu(WIDE, 0, 2)
+        gelu(WIDE, 0, 3)
         quantize_w2(0, 1)
-        hidden(WIDE, 0)
+        order_w1_codes(1)
+        order_w1_plane(1)
+        quantize_w2(0, 0)
+        order_w1_codes(2)
+        order_w1_plane(2)
         scale_hidden(NARROW, 0)
-        bias_product()
-        order_w1(2)
-        quantize_hidden(NARROW, 0)
+        hidden_matmul(WIDE, 1, 0)
+        hidden_matmul(WIDE, 1, 1)
+        hidden_matmul(WIDE, 1, 2)
+        hidden_matmul(WIDE, 1, 3)
         group_w2(1, 0, True)
-        hidden(WIDE, 1)
         scale_hidden(WIDE, 0)
-        order_w1(3)
+        quantize_hidden(NARROW, 0)
+        order_w1_codes(3)
+        order_w1_plane(3)
         quantize_hidden(WIDE, 0)
-        group_w2(1, 1, False)
+        hidden_matmul(WIDE, 2, 0)
+        hidden_matmul(WIDE, 2, 1)
+        hidden_matmul(WIDE, 2, 2)
+        hidden_matmul(WIDE, 2, 3)
+        gelu(WIDE, 1, 0)
+        gelu(WIDE, 1, 1)
+        gelu(WIDE, 1, 2)
+        gelu(WIDE, 1, 3)
+        group_w2(2, 0, False)
         quantize_w2(1, 0)
-        group_w2(2, 0, True)
-        hidden(WIDE, 2)
+        gelu(WIDE, 2, 0)
+        gelu(WIDE, 2, 1)
+        gelu(WIDE, 2, 2)
+        gelu(WIDE, 2, 3)
         scale_hidden(WIDE, 1)
-        quantize_w2(1, 1)
-        quantize_hidden(WIDE, 1)
-        quantize_w2(2, 0)
-        hidden(WIDE, 3)
-        scale_hidden(WIDE, 2)
+        hidden_matmul(WIDE, 3, 0)
+        hidden_matmul(WIDE, 3, 1)
+        hidden_matmul(WIDE, 3, 2)
+        hidden_matmul(WIDE, 3, 3)
         group_w2(3, 0, True)
-        quantize_hidden(WIDE, 2)
-        hidden(NARROW, 1)
-        scale_hidden(WIDE, 3)
+        scale_hidden(WIDE, 2)
+        quantize_w2(2, 0)
         quantize_w2(3, 0)
+        quantize_hidden(WIDE, 1)
+        gelu(WIDE, 3, 0)
+        gelu(WIDE, 3, 1)
+        gelu(WIDE, 3, 2)
+        gelu(WIDE, 3, 3)
+        hidden_matmul(NARROW, 1, 0)
+        hidden_matmul(NARROW, 1, 1)
+        hidden_matmul(NARROW, 2, 0)
+        hidden_matmul(NARROW, 2, 1)
+        group_w2(2, 1, True)
+        scale_hidden(WIDE, 3)
+        quantize_hidden(WIDE, 2)
+        bias_product()
         quantize_hidden(WIDE, 3)
-        hidden(NARROW, 2)
-        hidden(NARROW, 3)
+        gelu(NARROW, 1, 0)
+        gelu(NARROW, 1, 1)
+        hidden_matmul(NARROW, 3, 0)
+        hidden_matmul(NARROW, 3, 1)
+        gelu(NARROW, 2, 0)
+        gelu(NARROW, 2, 1)
+        group_w2(3, 1, True)
+        project(WIDE, 0, 0)
+        project(WIDE, 0, 1)
+        project(WIDE, 0, 2)
+        project(WIDE, 0, 3)
+        group_w2(1, 1, False)
+        quantize_w2(2, 1)
+        quantize_w2(1, 1)
+        quantize_w2(3, 1)
+        gelu(NARROW, 3, 0)
+        gelu(NARROW, 3, 1)
+        affine(WIDE, 0, 0, True)
+        affine(WIDE, 0, 1, True)
+        affine(WIDE, 0, 2, True)
+        affine(WIDE, 0, 3, True)
+        project(WIDE, 1, 0)
+        project(WIDE, 1, 1)
+        project(WIDE, 1, 2)
+        project(WIDE, 1, 3)
         scale_hidden(NARROW, 1)
         scale_hidden(NARROW, 2)
-        quantize_hidden(NARROW, 1)
-        group_w2(2, 1, True)
-        project(WIDE, 0)
         scale_hidden(NARROW, 3)
+        quantize_hidden(NARROW, 1)
         quantize_hidden(NARROW, 2)
-        group_w2(3, 1, False)
         quantize_hidden(NARROW, 3)
-        project(NARROW, 0)
-        quantize_w2(2, 1)
-        quantize_w2(3, 1)
-        rows_out(WIDE, 0)
+        affine(WIDE, 1, 0, True)
+        affine(WIDE, 1, 1, True)
+        affine(WIDE, 1, 2, True)
+        affine(WIDE, 1, 3, True)
+        cap_bank = turn_caption_weight()
+        caption_column(cap_bank, False)
+        turn(0, 0)
+        turn(1, 0)
+        turn(2, 0)
+        turn(3, 0)
+        rows_out(0, 0, True)
+        rows_out(1, 0, True)
+        turn(0, 1)
+        turn(1, 1)
+        rows_out(2, 0, True)
+        rows_out(3, 0, True)
+        turn(2, 1)
+        turn(3, 1)
         scale_y(WIDE, 0)
-        project(WIDE, 1)
-        rows_out(NARROW, 0)
-        scale_y(NARROW, 0)
+        rows_out(0, 1, True)
+        rows_out(1, 1, True)
+        project(NARROW, 0, 0)
+        project(NARROW, 0, 1)
+        scale_y(WIDE, 1)
         quantize_y(WIDE, 0)
+        affine(NARROW, 0, 0, True)
+        affine(NARROW, 0, 1, True)
+        rows_out(2, 1, True)
+        rows_out(3, 1, True)
+        quantize_y(WIDE, 1)
+        project(NARROW, 1, 0)
+        project(NARROW, 1, 1)
+        affine(NARROW, 1, 0, True)
+        affine(NARROW, 1, 1, True)
+        scale_y(NARROW, 0)
+        turn(4, 0)
+        turn(5, 0)
+        turn(4, 1)
+        turn(5, 1)
         quantize_y(NARROW, 0)
         store_plane(0)
-        scale_y(WIDE, 1)
-        rows_out(WIDE, 1)
-        project(NARROW, 1)
-        quantize_y(WIDE, 1)
+        rows_out(4, 0, False)
+        rows_out(5, 0, True)
         scale_y(NARROW, 1)
-        rows_out(NARROW, 1)
+        rows_out(4, 1, True)
+        rows_out(5, 1, True)
         quantize_y(NARROW, 1)
         store_plane(1)

@@ -55,13 +55,13 @@ def tile_caption_shared_embedding_h2_kernel(
         w1_plane_rest = kept("w1_plane_rest", [P, K_PASSES, F - GROUP], U8)
         w1_codes = [kept("w1_codes%d" % g, [P, PACK, K_PASSES, 2 * P], U8) for g in range(F_GROUPS)]
         w1_plane = [kept("w1_plane%d" % g, [P, PACK, K_PASSES, P], U8) for g in range(F_GROUPS)]
-        w2_raw = [kept("w2_raw%d" % g, [P, PACK, D], BF16) for g in range(F_GROUPS)]
+        w2_raw = {(g, h): kept("w2_raw%d%d" % (g, h), [P, PACK, GROUP], BF16) for g in range(F_GROUPS) for h in range(D_GROUPS)}
         w2_codes = {(g, h): kept("w2_codes%d%d" % (g, h), [P, GROUP], U32) for g in range(F_GROUPS) for h in range(D_GROUPS)}
         w2_plane = {(g, h): kept("w2_plane%d%d" % (g, h), [P, GROUP], U8) for g in range(F_GROUPS) for h in range(D_GROUPS)}
         h_codes = {(c, g): kept("h_codes%s%d" % (c, g), [P, CHUNK[c][1]], U32) for c in CHUNK for g in range(F_GROUPS)}
         h_plane = {(c, g): kept("h_plane%s%d" % (c, g), [P, CHUNK[c][1]], U8) for c in CHUNK for g in range(F_GROUPS)}
         y_codes = {(c, h): kept("y_codes%s%d" % (c, h), [P, CHUNK[c][1]], U32) for c in CHUNK for h in range(D_GROUPS)}
-        y_plane = [kept("y_plane%d" % h, [P, M], U8) for h in range(D_GROUPS)]
+        y_plane = kept("y_plane", [P, D_GROUPS, M], U8)
         gain_raw = kept("gain_raw", [F_GROUPS, GROUP], BF16)
         gain_rows = kept("gain_rows", [P, GROUP], F32)
         gain = kept("gain", [P, F_GROUPS, PACK], F32)
@@ -91,10 +91,11 @@ def tile_caption_shared_embedding_h2_kernel(
                     out=plane[32 * quad : 32 * quad + 4].bitcast(I32), in_=src[4 * quad : 4 * quad + 4].bitcast(I32)
                 )
 
-        def load_w2(g):
-            src = w2[GROUP * g : GROUP * (g + 1), :].rearrange("(q t r) n -> t q r n", t=PACK, r=8)
+        def load_w2(g, h):
+            src = w2[GROUP * g : GROUP * (g + 1), GROUP * h : GROUP * (h + 1)]
+            src = src.rearrange("(q t r) n -> t q r n", t=PACK, r=8)
             for t in range(PACK):
-                nc.sync.dma_start(out=w2_raw[g][:, t, :], in_=src[t])
+                nc.sync.dma_start(out=w2_raw[g, h][:, t, :], in_=src[t])
 
         def load_gain():
             nc.sync.dma_start(out=gain_raw[:], in_=hidden_scale.rearrange("(g f) -> g f", f=GROUP))
@@ -109,10 +110,9 @@ def tile_caption_shared_embedding_h2_kernel(
                 nc.tensor.transpose(bank[:, t, :], gain_rows[:, P * t : P * (t + 1)], ident[:])
             nc.scalar.copy(out=gain[:], in_=bank[:, :, 0:F_GROUPS].rearrange("p t g -> p g t"))
 
-        def load_late_vectors():
+        def load_channel_vectors():
             nc.sync.dma_start(out=b2_col[:], in_=b2.rearrange("(h p t) -> p h t", p=P, t=PACK))
             nc.sync.dma_start(out=dim_col[:], in_=dim_weight.rearrange("(h p t) -> p h t", p=P, t=PACK))
-            nc.sync.dma_start(out=cap_row[:], in_=caption_weight.partition_broadcast(P))
 
         nc.vector.memset(warm[:], 0.0)
         nc.scalar.activation(out=warm[:], in_=warm[:], func=ACT.Gelu_apprx_tanh)
@@ -128,16 +128,21 @@ def tile_caption_shared_embedding_h2_kernel(
         load_w1(0)
         load_plane(w1_plane_first, w1_scales[:, :, :GROUP])
         load_plane(x_plane, x_scales)
-        load_w2(0)
+        load_w2(0, 0)
         load_x(WIDE)
-        load_plane(w1_plane_rest, w1_scales[:, :, GROUP:])
         load_w1(1)
+        load_plane(w1_plane_rest, w1_scales[:, :, GROUP:])
         load_w1(2)
-        load_w2(1)
+        load_w2(1, 0)
         load_w1(3)
-        load_w2(2)
-        load_w2(3)
-        load_late_vectors()
+        load_w2(2, 1)
+        load_w2(2, 0)
+        load_w2(3, 0)
+        load_w2(0, 1)
+        load_channel_vectors()
+        load_w2(1, 1)
+        load_w2(3, 1)
+        nc.sync.dma_start(out=cap_row[:], in_=caption_weight.partition_broadcast(P))
         turn_gain()
 
         def turn_caption_weight():
@@ -220,17 +225,10 @@ def tile_caption_shared_embedding_h2_kernel(
             w = CHUNK[c][1]
             hb = work.tile([P, w, PACK], BF16, name="h_bf_%s%d" % (c, g), tag="bf", bufs=4, align_bytes=64)
             factor = gain[:, g, :]
+            act = gelu_of[c, g][:]
             if c == WIDE:
-                nc.vector.tensor_tensor(
-                    out=hb[:].rearrange("p (n i) t -> p n t i", i=2),
-                    in0=gelu_of[c, g][:].rearrange("p t (n i) -> p n t i", i=2),
-                    in1=factor.unsqueeze(1).unsqueeze(3).broadcast_to([P, w // 2, PACK, 2]),
-                    op=MULT,
-                )
-            else:
-                nc.vector.tensor_tensor(
-                    out=hb[:], in0=gelu_of[c, g][:], in1=factor.unsqueeze(1).broadcast_to([P, w, PACK]), op=MULT
-                )
+                act = act.rearrange("p t n -> p n t")
+            nc.vector.tensor_tensor(out=hb[:], in0=act, in1=factor.unsqueeze(1).broadcast_to([P, w, PACK]), op=MULT)
             h_bf[c, g] = hb
 
         def quantize(codes, plane, values):
@@ -245,8 +243,8 @@ def tile_caption_shared_embedding_h2_kernel(
 
         def group_w2(g, h, on_scalar):
             wb = work.tile([P, GROUP, PACK], BF16, name="w2_bf%d%d" % (g, h), tag="w2bf", bufs=6, align_bytes=64)
-            out = wb[:].rearrange("p (t m i) j -> p t m j i", t=PACK, i=2)
-            in_ = w2_raw[g][:, :, GROUP * h : GROUP * (h + 1)].rearrange("p j (m i t) -> p t m j i", t=PACK, i=2)
+            out = wb[:].rearrange("p (t m) j -> p t m j", t=PACK)
+            in_ = w2_raw[g, h][:].rearrange("p j (m t) -> p t m j", t=PACK)
             if on_scalar:
                 nc.scalar.copy(out=out, in_=in_)
             else:
@@ -316,36 +314,34 @@ def tile_caption_shared_embedding_h2_kernel(
         def scale_y(c, h):
             m0, w = CHUNK[c]
             yb = work.tile([P, w, PACK], BF16, name="y_bf_%s%d" % (c, h), tag="bf", bufs=4, align_bytes=64)
-            cap = cap_row[:, m0 : m0 + w].rearrange("p (n i) -> p n i", i=2)
             nc.vector.tensor_tensor(
-                out=yb[:].rearrange("p (n i) t -> p n t i", i=2),
-                in0=affine_of[c, h][:].rearrange("p t (n i) -> p n t i", i=2),
-                in1=cap.unsqueeze(2).broadcast_to([P, w // 2, PACK, 2]),
+                out=yb[:],
+                in0=affine_of[c, h][:].rearrange("p t n -> p n t"),
+                in1=cap_row[:, m0 : m0 + w].unsqueeze(2).broadcast_to([P, w, PACK]),
                 op=MULT,
             )
             y_bf[c, h] = yb
 
         def quantize_y(c, h):
             m0, w = CHUNK[c]
-            quantize(y_codes[c, h][:], y_plane[h][:, m0 : m0 + w], y_bf[c, h])
+            quantize(y_codes[c, h][:], y_plane[:, h, m0 : m0 + w], y_bf[c, h])
             dst = out_1[h].rearrange("p m t -> p (m t)")[:, 4 * m0 : 4 * (m0 + w)]
             nc.sync.dma_start(out=dst.bitcast(I32), in_=y_codes[c, h][:].bitcast(I32))
 
-        def store_plane(h):
+        def store_plane():
+            dst = out_2.rearrange("h q m -> q h m")
             for quad in range(4):
                 nc.sync.dma_start(
-                    out=out_2[h, 4 * quad : 4 * quad + 4, :].bitcast(I32),
-                    in_=y_plane[h][32 * quad : 32 * quad + 4, :].bitcast(I32),
+                    out=dst[4 * quad : 4 * quad + 4].bitcast(I32), in_=y_plane[32 * quad : 32 * quad + 4].bitcast(I32)
                 )
 
         order_w1_codes(0)
         order_w1_plane(0)
+        group_w2(0, 0, True)
         hidden_matmul(NARROW, 0, 0)
         hidden_matmul(NARROW, 0, 1)
-        group_w2(0, 1, True)
         gelu(NARROW, 0, 0)
         gelu(NARROW, 0, 1)
-        group_w2(0, 0, False)
         hidden_matmul(WIDE, 0, 0)
         hidden_matmul(WIDE, 0, 1)
         hidden_matmul(WIDE, 0, 2)
@@ -354,13 +350,12 @@ def tile_caption_shared_embedding_h2_kernel(
         gelu(WIDE, 0, 1)
         gelu(WIDE, 0, 2)
         gelu(WIDE, 0, 3)
-        quantize_w2(0, 1)
+        quantize_w2(0, 0)
         order_w1_codes(1)
         order_w1_plane(1)
-        quantize_w2(0, 0)
+        scale_hidden(NARROW, 0)
         order_w1_codes(2)
         order_w1_plane(2)
-        scale_hidden(NARROW, 0)
         hidden_matmul(WIDE, 1, 0)
         hidden_matmul(WIDE, 1, 1)
         hidden_matmul(WIDE, 1, 2)
@@ -379,50 +374,52 @@ def tile_caption_shared_embedding_h2_kernel(
         gelu(WIDE, 1, 1)
         gelu(WIDE, 1, 2)
         gelu(WIDE, 1, 3)
-        group_w2(2, 0, False)
-        quantize_w2(1, 0)
+        group_w2(2, 1, False)
         gelu(WIDE, 2, 0)
         gelu(WIDE, 2, 1)
         gelu(WIDE, 2, 2)
         gelu(WIDE, 2, 3)
         scale_hidden(WIDE, 1)
+        quantize_w2(1, 0)
         hidden_matmul(WIDE, 3, 0)
         hidden_matmul(WIDE, 3, 1)
         hidden_matmul(WIDE, 3, 2)
         hidden_matmul(WIDE, 3, 3)
-        group_w2(3, 0, True)
+        group_w2(2, 0, True)
         scale_hidden(WIDE, 2)
-        quantize_w2(2, 0)
-        quantize_w2(3, 0)
         quantize_hidden(WIDE, 1)
         gelu(WIDE, 3, 0)
         gelu(WIDE, 3, 1)
         gelu(WIDE, 3, 2)
         gelu(WIDE, 3, 3)
+        quantize_w2(2, 0)
         hidden_matmul(NARROW, 1, 0)
         hidden_matmul(NARROW, 1, 1)
         hidden_matmul(NARROW, 2, 0)
         hidden_matmul(NARROW, 2, 1)
-        group_w2(2, 1, True)
+        group_w2(3, 0, True)
         scale_hidden(WIDE, 3)
         quantize_hidden(WIDE, 2)
-        bias_product()
+        quantize_w2(3, 0)
         quantize_hidden(WIDE, 3)
         gelu(NARROW, 1, 0)
         gelu(NARROW, 1, 1)
         hidden_matmul(NARROW, 3, 0)
         hidden_matmul(NARROW, 3, 1)
+        group_w2(0, 1, True)
+        bias_product()
+        group_w2(3, 1, False)
+        group_w2(1, 1, True)
         gelu(NARROW, 2, 0)
         gelu(NARROW, 2, 1)
-        group_w2(3, 1, True)
         project(WIDE, 0, 0)
         project(WIDE, 0, 1)
         project(WIDE, 0, 2)
         project(WIDE, 0, 3)
-        group_w2(1, 1, False)
         quantize_w2(2, 1)
-        quantize_w2(1, 1)
+        quantize_w2(0, 1)
         quantize_w2(3, 1)
+        quantize_w2(1, 1)
         gelu(NARROW, 3, 0)
         gelu(NARROW, 3, 1)
         affine(WIDE, 0, 0, True)
@@ -435,8 +432,8 @@ def tile_caption_shared_embedding_h2_kernel(
         project(WIDE, 1, 3)
         scale_hidden(NARROW, 1)
         scale_hidden(NARROW, 2)
-        scale_hidden(NARROW, 3)
         quantize_hidden(NARROW, 1)
+        scale_hidden(NARROW, 3)
         quantize_hidden(NARROW, 2)
         quantize_hidden(NARROW, 3)
         affine(WIDE, 1, 0, True)
@@ -444,46 +441,45 @@ def tile_caption_shared_embedding_h2_kernel(
         affine(WIDE, 1, 2, True)
         affine(WIDE, 1, 3, True)
         cap_bank = turn_caption_weight()
-        caption_column(cap_bank, False)
+        caption_column(cap_bank, True)
         turn(0, 0)
         turn(1, 0)
         turn(2, 0)
         turn(3, 0)
         rows_out(0, 0, True)
         rows_out(1, 0, True)
-        turn(0, 1)
-        turn(1, 1)
-        rows_out(2, 0, True)
-        rows_out(3, 0, True)
-        turn(2, 1)
-        turn(3, 1)
-        scale_y(WIDE, 0)
-        rows_out(0, 1, True)
-        rows_out(1, 1, True)
         project(NARROW, 0, 0)
         project(NARROW, 0, 1)
-        scale_y(WIDE, 1)
-        quantize_y(WIDE, 0)
+        rows_out(2, 0, True)
+        rows_out(3, 0, True)
+        scale_y(WIDE, 0)
         affine(NARROW, 0, 0, True)
         affine(NARROW, 0, 1, True)
-        rows_out(2, 1, True)
-        rows_out(3, 1, True)
-        quantize_y(WIDE, 1)
-        project(NARROW, 1, 0)
-        project(NARROW, 1, 1)
-        affine(NARROW, 1, 0, True)
-        affine(NARROW, 1, 1, True)
-        scale_y(NARROW, 0)
+        turn(0, 1)
+        turn(1, 1)
+        turn(2, 1)
+        turn(3, 1)
         turn(4, 0)
         turn(5, 0)
+        scale_y(WIDE, 1)
+        rows_out(0, 1, True)
+        rows_out(1, 1, True)
+        rows_out(2, 1, True)
+        rows_out(3, 1, True)
+        project(NARROW, 1, 0)
+        project(NARROW, 1, 1)
+        quantize_y(WIDE, 0)
+        scale_y(NARROW, 0)
+        quantize_y(WIDE, 1)
+        affine(NARROW, 1, 0, True)
+        affine(NARROW, 1, 1, True)
+        quantize_y(NARROW, 0)
+        rows_out(4, 0, True)
+        rows_out(5, 0, True)
         turn(4, 1)
         turn(5, 1)
-        quantize_y(NARROW, 0)
-        store_plane(0)
-        rows_out(4, 0, False)
-        rows_out(5, 0, True)
         scale_y(NARROW, 1)
         rows_out(4, 1, True)
         rows_out(5, 1, True)
         quantize_y(NARROW, 1)
-        store_plane(1)
+        store_plane()

@@ -15,17 +15,25 @@ FP8X4 = mybir.dt.float8_e4m3fn_x4
 FP4X4 = mybir.dt.float4_e2m1fn_x4
 ACT = mybir.ActivationFunctionType
 MULT = mybir.AluOpType.mult
-ADD = mybir.AluOpType.add
 
 P = 128
-PACK = 4
-GROUP = P * PACK
-K_PASSES = K // GROUP
-F_GROUPS = F // GROUP
-D_GROUPS = D // GROUP
+SLOTS = 4
+SPAN = P * SLOTS
+RUN = 8
+K_PASSES = K // SPAN
+F_GROUPS = F // SPAN
+D_HALVES = D // SPAN
 BANKS = 8
+BANK_COLUMNS = 512
+QUADRANT = 32
+SCALE_ROWS = 4
+
 WIDE, NARROW = "wide", "narrow"
-CHUNK = {WIDE: (0, 512), NARROW: (512, 256)}
+CHUNK = {WIDE: (0, BANK_COLUMNS), NARROW: (BANK_COLUMNS, M - BANK_COLUMNS)}
+WIDE_TILES = range(0, BANK_COLUMNS // P)
+NARROW_TILES = range(BANK_COLUMNS // P, M // P)
+
+F32_BUFS, SCALED_BUFS, GROUPED_BUFS, W2_GROUPED_BUFS, ROW_BUFS = 4, 3, 4, 6, 6
 
 
 def tile_caption_shared_embedding_h2_kernel(
@@ -34,88 +42,68 @@ def tile_caption_shared_embedding_h2_kernel(
     nc = tc.nc
     with ExitStack() as ctx:
         keep = ctx.enter_context(tc.tile_pool(name="keep", bufs=1))
-        work = ctx.enter_context(tc.tile_pool(name="work", bufs=3))
+        work = ctx.enter_context(tc.tile_pool(name="work", bufs=1))
         psum = ctx.enter_context(tc.psum_pool(name="psum", bufs=1))
         ctx.enter_context(tc.manual_schedule())
 
         banks_used = []
 
-        def next_bank(shape, dtype=F32):
-            n = len(banks_used)
-            banks_used.append(n)
-            return psum.tile(shape, dtype, name="bank_%d" % n, tag="bank%d" % (n % BANKS))
+        def next_bank(shape, dtype):
+            count = len(banks_used)
+            banks_used.append(count)
+            return psum.tile(shape, dtype, name="bank_%d" % count, tag="bank%d" % (count % BANKS))
 
         def kept(name, shape, dtype):
             return keep.tile(shape, dtype, name=name, align_bytes=64)
 
+        groups = range(F_GROUPS)
+        halves = range(D_HALVES)
         x_codes = {c: kept("x_codes_" + c, [P, K_PASSES, CHUNK[c][1]], I32) for c in CHUNK}
         x_plane = kept("x_plane", [P, K_PASSES, M], U8)
-        w1_raw = [kept("w1_raw%d" % g, [P, K_PASSES, 256], I32) for g in range(F_GROUPS)]
-        w1_plane_first = kept("w1_plane_first", [P, K_PASSES, GROUP], U8)
-        w1_plane_rest = kept("w1_plane_rest", [P, K_PASSES, F - GROUP], U8)
-        w1_codes = [kept("w1_codes%d" % g, [P, PACK, K_PASSES, 2 * P], U8) for g in range(F_GROUPS)]
-        w1_plane = [kept("w1_plane%d" % g, [P, PACK, K_PASSES, P], U8) for g in range(F_GROUPS)]
-        w2_raw = {(g, h): kept("w2_raw%d%d" % (g, h), [P, PACK, GROUP], BF16) for g in range(F_GROUPS) for h in range(D_GROUPS)}
-        w2_codes = {(g, h): kept("w2_codes%d%d" % (g, h), [P, GROUP], U32) for g in range(F_GROUPS) for h in range(D_GROUPS)}
-        w2_plane = {(g, h): kept("w2_plane%d%d" % (g, h), [P, GROUP], U8) for g in range(F_GROUPS) for h in range(D_GROUPS)}
-        h_codes = {(c, g): kept("h_codes%s%d" % (c, g), [P, CHUNK[c][1]], U32) for c in CHUNK for g in range(F_GROUPS)}
-        h_plane = {(c, g): kept("h_plane%s%d" % (c, g), [P, CHUNK[c][1]], U8) for c in CHUNK for g in range(F_GROUPS)}
-        y_codes = {(c, h): kept("y_codes%s%d" % (c, h), [P, CHUNK[c][1]], U32) for c in CHUNK for h in range(D_GROUPS)}
-        y_plane = kept("y_plane", [P, D_GROUPS, M], U8)
-        gain_raw = kept("gain_raw", [F_GROUPS, GROUP], BF16)
-        gain_rows = kept("gain_rows", [P, GROUP], F32)
-        gain = kept("gain", [P, F_GROUPS, PACK], F32)
-        b2_col = kept("b2_col", [P, D_GROUPS, PACK], BF16)
-        dim_col = kept("dim_col", [P, D_GROUPS, PACK], BF16)
-        dim_f32 = kept("dim_f32", [P, D_GROUPS, PACK], F32)
-        bias = kept("bias", [P, D_GROUPS, PACK], F32)
+        w1_raw = [kept("w1_raw%d" % g, [P, K_PASSES, SPAN // 2], I32) for g in groups]
+        w1_plane_first = kept("w1_plane_first", [P, K_PASSES, SPAN], U8)
+        w1_plane_rest = kept("w1_plane_rest", [P, K_PASSES, F - SPAN], U8)
+        w1_codes = [kept("w1_codes%d" % g, [P, SLOTS, K_PASSES, 2 * P], U8) for g in groups]
+        w1_plane = [kept("w1_plane%d" % g, [P, SLOTS, K_PASSES, P], U8) for g in groups]
+        w2_raw = {(g, h): kept("w2_raw%d%d" % (g, h), [P, SLOTS, SPAN], BF16) for g in groups for h in halves}
+        w2_codes = {(g, h): kept("w2_codes%d%d" % (g, h), [P, SPAN], U32) for g in groups for h in halves}
+        w2_plane = {(g, h): kept("w2_plane%d%d" % (g, h), [P, SPAN], U8) for g in groups for h in halves}
+        h_codes = {(c, g): kept("h_codes%s%d" % (c, g), [P, CHUNK[c][1]], U32) for c in CHUNK for g in groups}
+        h_plane = {(c, g): kept("h_plane%s%d" % (c, g), [P, CHUNK[c][1]], U8) for c in CHUNK for g in groups}
+        y_codes = {(c, h): kept("y_codes%s%d" % (c, h), [P, CHUNK[c][1]], U32) for c in CHUNK for h in halves}
+        y_plane = kept("y_plane", [P, D_HALVES, M], U8)
+        gain_raw = kept("gain_raw", [F_GROUPS, SPAN], BF16)
+        gain_rows = kept("gain_rows", [P, SPAN], F32)
+        gain = kept("gain", [P, F_GROUPS, SLOTS], F32)
+        b2_col = kept("b2_col", [P, D_HALVES, SLOTS], BF16)
+        dim_col = kept("dim_col", [P, D_HALVES, SLOTS], BF16)
+        dim_f32 = kept("dim_f32", [P, D_HALVES, SLOTS], F32)
+        bias = kept("bias", [P, D_HALVES, SLOTS], F32)
         cap_row = kept("cap_row", [P, M], BF16)
         cap_col = kept("cap_col", [P, M // P], F32)
         ident = kept("ident", [P, P], F32)
         ident_bf = kept("ident_bf", [P, P], BF16)
-        warm = kept("warm", [P, 1], F32)
 
         def load_x(c):
-            m0, w = CHUNK[c]
-            src = x_words.rearrange("c p m t -> p c (m t)")[:, :, 4 * m0 : 4 * (m0 + w)]
+            m0, width = CHUNK[c]
+            src = x_words.rearrange("k p m t -> p k (m t)")[:, :, SLOTS * m0 : SLOTS * (m0 + width)]
             nc.sync.dma_start(out=x_codes[c][:], in_=src.bitcast(I32))
 
         def load_w1(g):
-            src = w1_words.rearrange("c p n -> p c n")[:, :, 1024 * g : 1024 * (g + 1)]
+            src = w1_words.rearrange("k p n -> p k n")[:, :, 2 * SPAN * g : 2 * SPAN * (g + 1)]
             nc.sync.dma_start(out=w1_raw[g][:], in_=src.bitcast(I32))
 
         def load_plane(plane, scales):
-            src = scales.rearrange("c q n -> q c n")
-            for quad in range(4):
-                nc.sync.dma_start(
-                    out=plane[32 * quad : 32 * quad + 4].bitcast(I32), in_=src[4 * quad : 4 * quad + 4].bitcast(I32)
-                )
+            src = scales.rearrange("k q n -> q k n")
+            for r in range(SCALE_ROWS):
+                nc.sync.dma_start(out=plane[r:P:QUADRANT].bitcast(I32), in_=src[r : P // RUN : SCALE_ROWS].bitcast(I32))
 
         def load_w2(g, h):
-            src = w2[GROUP * g : GROUP * (g + 1), GROUP * h : GROUP * (h + 1)]
-            src = src.rearrange("(q t r) n -> t q r n", t=PACK, r=8)
-            for t in range(PACK):
+            src = w2[SPAN * g : SPAN * (g + 1), SPAN * h : SPAN * (h + 1)]
+            src = src.rearrange("(q t r) n -> t q r n", t=SLOTS, r=RUN)
+            for t in range(SLOTS):
                 nc.sync.dma_start(out=w2_raw[g, h][:, t, :], in_=src[t])
 
-        def load_gain():
-            nc.sync.dma_start(out=gain_raw[:], in_=hidden_scale.rearrange("(g f) -> g f", f=GROUP))
-
-        def turn_gain():
-            nc.scalar.copy(
-                out=gain_rows[0:F_GROUPS, :].rearrange("g (t q r) -> g t q r", t=PACK, r=8),
-                in_=gain_raw[:].rearrange("g (q t r) -> g t q r", t=PACK, r=8),
-            )
-            bank = next_bank([P, PACK, P])
-            for t in range(PACK):
-                nc.tensor.transpose(bank[:, t, :], gain_rows[:, P * t : P * (t + 1)], ident[:])
-            nc.scalar.copy(out=gain[:], in_=bank[:, :, 0:F_GROUPS].rearrange("p t g -> p g t"))
-
-        def load_channel_vectors():
-            nc.sync.dma_start(out=b2_col[:], in_=b2.rearrange("(h p t) -> p h t", p=P, t=PACK))
-            nc.sync.dma_start(out=dim_col[:], in_=dim_weight.rearrange("(h p t) -> p h t", p=P, t=PACK))
-
-        nc.vector.memset(warm[:], 0.0)
-        nc.scalar.activation(out=warm[:], in_=warm[:], func=ACT.Gelu_apprx_tanh)
         nc.vector.memset(w1_plane_first[:].bitcast(I32), 0)
         nc.vector.memset(x_plane[:].bitcast(I32), 0)
         nc.vector.memset(ident[:], 0.0)
@@ -123,15 +111,15 @@ def tile_caption_shared_embedding_h2_kernel(
         nc.vector.memset(gain_rows[:], 0.0)
         nc.vector.memset(w1_plane_rest[:].bitcast(I32), 0)
 
-        load_gain()
+        nc.sync.dma_start(out=gain_raw[:], in_=hidden_scale.rearrange("(g f) -> g f", f=SPAN))
         load_x(NARROW)
         load_w1(0)
-        load_plane(w1_plane_first, w1_scales[:, :, :GROUP])
+        load_plane(w1_plane_first, w1_scales[:, :, :SPAN])
         load_plane(x_plane, x_scales)
         load_w2(0, 0)
         load_x(WIDE)
         load_w1(1)
-        load_plane(w1_plane_rest, w1_scales[:, :, GROUP:])
+        load_plane(w1_plane_rest, w1_scales[:, :, SPAN:])
         load_w1(2)
         load_w2(1, 0)
         load_w1(3)
@@ -139,33 +127,37 @@ def tile_caption_shared_embedding_h2_kernel(
         load_w2(2, 0)
         load_w2(3, 0)
         load_w2(0, 1)
-        load_channel_vectors()
+        nc.sync.dma_start(out=b2_col[:], in_=b2.rearrange("(h p t) -> p h t", p=P, t=SLOTS))
+        nc.sync.dma_start(out=dim_col[:], in_=dim_weight.rearrange("(h p t) -> p h t", p=P, t=SLOTS))
         load_w2(1, 1)
         load_w2(3, 1)
         nc.sync.dma_start(out=cap_row[:], in_=caption_weight.partition_broadcast(P))
-        turn_gain()
 
-        def turn_caption_weight():
-            bank = next_bank([P, M // P, P], BF16)
-            for mt in range(M // P):
-                nc.tensor.transpose(bank[:, mt, :], cap_row[:, P * mt : P * (mt + 1)], ident_bf[:])
-            return bank
+        def place_gain():
+            nc.scalar.copy(
+                out=gain_rows[0:F_GROUPS, :].rearrange("g (t q r) -> g t q r", t=SLOTS, r=RUN),
+                in_=gain_raw[:].rearrange("g (q t r) -> g t q r", t=SLOTS, r=RUN),
+            )
+            bank = next_bank([P, SLOTS, P], F32)
+            for t in range(SLOTS):
+                nc.tensor.transpose(bank[:, t, :], gain_rows[:, P * t : P * (t + 1)], ident[:])
+            nc.scalar.copy(out=gain[:], in_=bank[:, :, 0:F_GROUPS].rearrange("p t g -> p g t"))
 
-        def caption_column(bank, on_scalar):
-            if on_scalar:
-                nc.scalar.copy(out=cap_col[:], in_=bank[:, :, 0])
-            else:
-                nc.vector.tensor_copy(out=cap_col[:], in_=bank[:, :, 0])
-
-        def bias_product():
+        def prepare_epilogue_constants():
             nc.vector.tensor_copy(out=ident_bf[:], in_=ident[:])
             nc.vector.tensor_copy(out=dim_f32[:], in_=dim_col[:])
             nc.vector.tensor_tensor(out=bias[:], in0=b2_col[:], in1=dim_col[:], op=MULT)
 
+        def place_caption_weight():
+            bank = next_bank([P, M // P, P], BF16)
+            for i in range(M // P):
+                nc.tensor.transpose(bank[:, i, :], cap_row[:, P * i : P * (i + 1)], ident_bf[:])
+            nc.scalar.copy(out=cap_col[:], in_=bank[:, :, 0])
+
         def order_w1_codes(g):
             nc.vector.tensor_copy(
-                out=w1_codes[g][:].bitcast(I32).rearrange("p t c (q w) -> p t (c q) w", w=4),
-                in_=w1_raw[g][:].rearrange("p c (q t w) -> p t (c q) w", t=PACK, w=4),
+                out=w1_codes[g][:].bitcast(I32).rearrange("p t k (q w) -> p t (k q) w", w=RUN // 2),
+                in_=w1_raw[g][:].rearrange("p k (q t w) -> p t (k q) w", t=SLOTS, w=RUN // 2),
             )
 
         def order_w1_plane(g):
@@ -174,98 +166,109 @@ def tile_caption_shared_embedding_h2_kernel(
             else:
                 src = w1_plane_rest[:].bitcast(I32)[:, :, P * (g - 1) : P * g]
             nc.vector.tensor_copy(
-                out=w1_plane[g][:].bitcast(I32).rearrange("p t c (q w) -> p t c q w", w=2),
-                in_=src.rearrange("p c (q t w) -> p t c q w", t=PACK, w=2),
+                out=w1_plane[g][:].bitcast(I32).rearrange("p t k (q w) -> p t k q w", w=RUN // 4),
+                in_=src.rearrange("p k (q t w) -> p t k q w", t=SLOTS, w=RUN // 4),
             )
 
-        gelu_of = {}
-        h_bf = {}
+        u_banks, gelu_of, scaled_of, h_grouped = {}, {}, {}, {}
 
-        bank_of = {}
+        def hidden_matmuls(c, g):
+            m0, width = CHUNK[c]
 
-        def hidden_matmul(c, g, u):
-            m0, w = CHUNK[c]
-
-            def passes(out, t, lo, n):
+            def passes(out, t, first, count):
                 for k in range(K_PASSES):
                     nc.tensor.matmul_mx(
                         out=out,
                         lhsT=w1_codes[g][:, t, k, :].bitcast(FP4X4),
                         lhsT_scale=w1_plane[g][:, t, k, :],
-                        rhs=x_codes[c][:, k, lo : lo + n].bitcast(FP8X4),
-                        rhs_scale=x_plane[:, k, m0 + lo : m0 + lo + n],
+                        rhs=x_codes[c][:, k, first : first + count].bitcast(FP8X4),
+                        rhs_scale=x_plane[:, k, m0 + first : m0 + first + count],
                         start=(k == 0),
                         stop=(k == K_PASSES - 1),
                     )
 
+            u_banks[c, g] = []
             if c == WIDE:
-                bank = next_bank([P, w])
-                passes(bank[:], u, 0, w)
+                for t in range(SLOTS):
+                    bank = next_bank([P, width], F32)
+                    passes(bank[:], t, 0, width)
+                    u_banks[c, g].append(bank)
             else:
-                bank = next_bank([P, PACK, P])
-                for t in range(PACK):
-                    passes(bank[:, t, :], t, P * u, P)
-            bank_of["hidden", c, g, u] = bank
+                for first in range(0, width, P):
+                    bank = next_bank([P, SLOTS, P], F32)
+                    for t in range(SLOTS):
+                        passes(bank[:, t, :], t, first, P)
+                    u_banks[c, g].append(bank)
 
-        def gelu(c, g, u):
-            w = CHUNK[c][1]
-            bank = bank_of["hidden", c, g, u]
-            if (c, g) not in gelu_of:
-                shape = [P, PACK, w] if c == WIDE else [P, w, PACK]
-                gelu_of[c, g] = work.tile(shape, F32, name="gelu_%s%d" % (c, g), tag="f32", bufs=5)
-            act = gelu_of[c, g]
-            if c == WIDE:
-                nc.scalar.activation(out=act[:, u, :], in_=bank[:], func=ACT.Gelu_apprx_tanh)
-            else:
-                nc.scalar.activation(
-                    out=act[:, P * u : P * (u + 1), :], in_=bank[:].rearrange("p t m -> p m t"), func=ACT.Gelu_apprx_tanh
+        def gelu(c, g):
+            width = CHUNK[c][1]
+            shape = [P, SLOTS, width] if c == WIDE else [P, width, SLOTS]
+            values = work.tile(shape, F32, name="gelu_%s%d" % (c, g), tag="f32", bufs=F32_BUFS)
+            for i, bank in enumerate(u_banks[c, g]):
+                if c == WIDE:
+                    out, src = values[:, i, :], bank[:]
+                else:
+                    out, src = values[:, P * i : P * (i + 1), :], bank[:].rearrange("p t m -> p m t")
+                nc.scalar.activation(out=out, in_=src, func=ACT.Gelu_apprx_tanh)
+            gelu_of[c, g] = values
+
+        def grouped_tile(name, width):
+            return work.tile([P, width, SLOTS], BF16, name=name, tag="grouped", bufs=GROUPED_BUFS, align_bytes=64)
+
+        def scale_narrow(g):
+            width = CHUNK[NARROW][1]
+            grouped = grouped_tile("h_narrow%d" % g, width)
+            factor = gain[:, g, :].unsqueeze(1).broadcast_to([P, width, SLOTS])
+            nc.vector.tensor_tensor(out=grouped[:], in0=gelu_of[NARROW, g][:], in1=factor, op=MULT)
+            h_grouped[NARROW, g] = grouped
+
+        def scale_wide(g):
+            scaled = work.tile([P, SLOTS, CHUNK[WIDE][1]], BF16, name="scaled%d" % g, tag="scaled", bufs=SCALED_BUFS)
+            for t in range(SLOTS):
+                nc.vector.tensor_scalar(
+                    out=scaled[:, t, :], in0=gelu_of[WIDE, g][:, t, :], scalar1=gain[:, g, t : t + 1], scalar2=None, op0=MULT
                 )
+            scaled_of[g] = scaled
 
-        def scale_hidden(c, g):
-            w = CHUNK[c][1]
-            hb = work.tile([P, w, PACK], BF16, name="h_bf_%s%d" % (c, g), tag="bf", bufs=4, align_bytes=64)
-            factor = gain[:, g, :]
-            act = gelu_of[c, g][:]
-            if c == WIDE:
-                act = act.rearrange("p t n -> p n t")
-            nc.vector.tensor_tensor(out=hb[:], in0=act, in1=factor.unsqueeze(1).broadcast_to([P, w, PACK]), op=MULT)
-            h_bf[c, g] = hb
+        def group_wide(g):
+            grouped = grouped_tile("h_wide%d" % g, CHUNK[WIDE][1])
+            nc.vector.tensor_copy(out=grouped[:], in_=scaled_of[g][:].rearrange("p t m -> p m t"))
+            h_grouped[WIDE, g] = grouped
 
-        def quantize(codes, plane, values):
-            nc.vector.quantize_mx(
-                out=codes.bitcast(FP8X4), scales=plane, in_=values[:].rearrange("p n t -> p (n t)")
+        def quantize(codes, plane, grouped):
+            nc.vector.quantize_mx(out=codes.bitcast(FP8X4), scales=plane, in_=grouped[:].rearrange("p n t -> p (n t)"))
+
+        def quantize_h(c, g):
+            quantize(h_codes[c, g][:], h_plane[c, g][:], h_grouped[c, g])
+
+        w2_grouped = {}
+
+        def group_w2(g, h, copy):
+            grouped = work.tile(
+                [P, SPAN, SLOTS], BF16, name="w2_grouped%d%d" % (g, h), tag="w2_grouped", bufs=W2_GROUPED_BUFS, align_bytes=64
             )
-
-        def quantize_hidden(c, g):
-            quantize(h_codes[c, g][:], h_plane[c, g][:], h_bf[c, g])
-
-        w2_bf = {}
-
-        def group_w2(g, h, on_scalar):
-            wb = work.tile([P, GROUP, PACK], BF16, name="w2_bf%d%d" % (g, h), tag="w2bf", bufs=6, align_bytes=64)
-            out = wb[:].rearrange("p (t m) j -> p t m j", t=PACK)
-            in_ = w2_raw[g, h][:].rearrange("p j (m t) -> p t m j", t=PACK)
-            if on_scalar:
-                nc.scalar.copy(out=out, in_=in_)
-            else:
-                nc.vector.tensor_copy(out=out, in_=in_)
-            w2_bf[g, h] = wb
+            copy(
+                out=grouped[:].rearrange("p (t n) j -> p n j t", t=SLOTS),
+                in_=w2_raw[g, h][:].rearrange("p j (n t) -> p n j t", t=SLOTS),
+            )
+            w2_grouped[g, h] = grouped
 
         def quantize_w2(g, h):
-            quantize(w2_codes[g, h][:], w2_plane[g, h][:], w2_bf[g, h])
+            quantize(w2_codes[g, h][:], w2_plane[g, h][:], w2_grouped[g, h])
 
-        affine_of = {}
-        y_bf = {}
+        z_banks, affine_of, turned, y_grouped = {}, {}, {}, {}
 
-        def project(c, h, u):
-            w = CHUNK[c][1]
-            per_bank = 512 // w
-            bank = next_bank([P, per_bank, w])
-            for s in range(per_bank):
-                t = per_bank * u + s
-                for g in range(F_GROUPS):
+        def project(c, h):
+            width = CHUNK[c][1]
+            per_bank = BANK_COLUMNS // width
+            z_banks[c, h] = []
+            for t in range(SLOTS):
+                if t % per_bank == 0:
+                    bank = next_bank([P, per_bank, width], F32)
+                out = bank[:, t % per_bank, :]
+                for g in groups:
                     nc.tensor.matmul_mx(
-                        out=bank[:, s, :],
+                        out=out,
                         lhsT=w2_codes[g, h][:, P * t : P * (t + 1)].bitcast(FP8X4),
                         lhsT_scale=w2_plane[g, h][:, P * t : P * (t + 1)],
                         rhs=h_codes[c, g][:].bitcast(FP8X4),
@@ -273,213 +276,159 @@ def tile_caption_shared_embedding_h2_kernel(
                         start=(g == 0),
                         stop=(g == F_GROUPS - 1),
                     )
-            bank_of["project", c, h, u] = bank
+                z_banks[c, h].append(out)
 
-        def affine(c, h, u, on_scalar):
-            w = CHUNK[c][1]
-            per_bank = 512 // w
-            bank = bank_of["project", c, h, u]
-            if (c, h) not in affine_of:
-                affine_of[c, h] = work.tile([P, PACK, w], F32, name="aff_%s%d" % (c, h), tag="f32", bufs=5)
-            for s in range(per_bank):
-                t = per_bank * u + s
-                scale = dim_f32[:, h, t : t + 1]
-                shift = bias[:, h, t : t + 1]
-                out = affine_of[c, h][:, t, :]
-                if on_scalar:
-                    nc.scalar.activation(out=out, in_=bank[:, s, :], func=ACT.Identity, scale=scale, bias=shift)
-                else:
-                    nc.vector.tensor_scalar(out=out, in0=bank[:, s, :], scalar1=scale, scalar2=shift, op0=MULT, op1=ADD)
+        def affine(c, h):
+            values = work.tile([P, SLOTS, CHUNK[c][1]], F32, name="affine_%s%d" % (c, h), tag="f32", bufs=F32_BUFS)
+            for t in range(SLOTS):
+                nc.scalar.activation(
+                    out=values[:, t, :],
+                    in_=z_banks[c, h][t],
+                    func=ACT.Identity,
+                    scale=dim_f32[:, h, t : t + 1],
+                    bias=bias[:, h, t : t + 1],
+                )
+            affine_of[c, h] = values
 
-        def turn(mt, h):
-            c = WIDE if P * mt < CHUNK[NARROW][0] else NARROW
-            lo = P * mt - CHUNK[c][0]
-            bank = next_bank([P, PACK, P])
-            for t in range(PACK):
-                nc.tensor.transpose(bank[:, t, :], affine_of[c, h][:, t, lo : lo + P], ident[:])
-            bank_of["turn", mt, h] = bank
+        def turn(tiles, h):
+            for i in tiles:
+                c = WIDE if i in WIDE_TILES else NARROW
+                first = P * i - CHUNK[c][0]
+                bank = next_bank([P, SLOTS, P], F32)
+                for t in range(SLOTS):
+                    nc.tensor.transpose(bank[:, t, :], affine_of[c, h][:, t, first : first + P], ident[:])
+                turned[i, h] = bank
 
-        def rows_out(mt, h, on_scalar):
-            y = work.tile([P, P, PACK], F32, name="y_%d%d" % (mt, h), tag="y", bufs=6)
-            cap = cap_col[:, mt : mt + 1]
-            src = bank_of["turn", mt, h][:].rearrange("m t p -> m p t")
-            if on_scalar:
-                nc.scalar.activation(out=y[:], in_=src, func=ACT.Copy, scale=cap)
-            else:
-                nc.vector.tensor_scalar(out=y[:], in0=src, scalar1=cap, scalar2=None, op0=MULT)
-            nc.sync.dma_start(
-                out=out_0[P * mt : P * (mt + 1), GROUP * h : GROUP * (h + 1)], in_=y[:].rearrange("m p t -> m (p t)")
-            )
-
-        def scale_y(c, h):
-            m0, w = CHUNK[c]
-            yb = work.tile([P, w, PACK], BF16, name="y_bf_%s%d" % (c, h), tag="bf", bufs=4, align_bytes=64)
-            nc.vector.tensor_tensor(
-                out=yb[:],
-                in0=affine_of[c, h][:].rearrange("p t n -> p n t"),
-                in1=cap_row[:, m0 : m0 + w].unsqueeze(2).broadcast_to([P, w, PACK]),
-                op=MULT,
-            )
-            y_bf[c, h] = yb
-
-        def quantize_y(c, h):
-            m0, w = CHUNK[c]
-            quantize(y_codes[c, h][:], y_plane[:, h, m0 : m0 + w], y_bf[c, h])
-            dst = out_1[h].rearrange("p m t -> p (m t)")[:, 4 * m0 : 4 * (m0 + w)]
-            nc.sync.dma_start(out=dst.bitcast(I32), in_=y_codes[c, h][:].bitcast(I32))
-
-        def store_plane():
-            dst = out_2.rearrange("h q m -> q h m")
-            for quad in range(4):
+        def store_rows(tiles, h):
+            for i in tiles:
+                rows = work.tile([P, P, SLOTS], F32, name="rows_%d%d" % (i, h), tag="rows", bufs=ROW_BUFS)
+                nc.scalar.activation(
+                    out=rows[:], in_=turned[i, h][:].rearrange("m t p -> m p t"), func=ACT.Copy, scale=cap_col[:, i : i + 1]
+                )
                 nc.sync.dma_start(
-                    out=dst[4 * quad : 4 * quad + 4].bitcast(I32), in_=y_plane[32 * quad : 32 * quad + 4].bitcast(I32)
+                    out=out_0[P * i : P * (i + 1), SPAN * h : SPAN * (h + 1)], in_=rows[:].rearrange("m p t -> m (p t)")
                 )
 
+        def scale_y(c, h):
+            m0, width = CHUNK[c]
+            grouped = grouped_tile("y_%s%d" % (c, h), width)
+            nc.vector.tensor_tensor(
+                out=grouped[:],
+                in0=affine_of[c, h][:].rearrange("p t m -> p m t"),
+                in1=cap_row[:, m0 : m0 + width].unsqueeze(2).broadcast_to([P, width, SLOTS]),
+                op=MULT,
+            )
+            y_grouped[c, h] = grouped
+
+        def quantize_y(c, h):
+            m0, width = CHUNK[c]
+            quantize(y_codes[c, h][:], y_plane[:, h, m0 : m0 + width], y_grouped[c, h])
+            dst = out_1[h].rearrange("p m t -> p (m t)")[:, SLOTS * m0 : SLOTS * (m0 + width)]
+            nc.sync.dma_start(out=dst.bitcast(I32), in_=y_codes[c, h][:].bitcast(I32))
+
+        def store_y_plane():
+            dst = out_2.rearrange("h q m -> q h m")
+            for r in range(SCALE_ROWS):
+                nc.sync.dma_start(out=dst[r : P // RUN : SCALE_ROWS].bitcast(I32), in_=y_plane[r:P:QUADRANT].bitcast(I32))
+
+        on_vector, on_scalar = nc.vector.tensor_copy, nc.scalar.copy
+
+        place_gain()
         order_w1_codes(0)
         order_w1_plane(0)
-        group_w2(0, 0, True)
-        hidden_matmul(NARROW, 0, 0)
-        hidden_matmul(NARROW, 0, 1)
-        gelu(NARROW, 0, 0)
-        gelu(NARROW, 0, 1)
-        hidden_matmul(WIDE, 0, 0)
-        hidden_matmul(WIDE, 0, 1)
-        hidden_matmul(WIDE, 0, 2)
-        hidden_matmul(WIDE, 0, 3)
-        gelu(WIDE, 0, 0)
-        gelu(WIDE, 0, 1)
-        gelu(WIDE, 0, 2)
-        gelu(WIDE, 0, 3)
-        quantize_w2(0, 0)
+        hidden_matmuls(NARROW, 0)
+        gelu(NARROW, 0)
+        group_w2(0, 0, on_vector)
+
+        hidden_matmuls(WIDE, 0)
+        gelu(WIDE, 0)
         order_w1_codes(1)
+        quantize_w2(0, 0)
         order_w1_plane(1)
-        scale_hidden(NARROW, 0)
+        scale_narrow(0)
         order_w1_codes(2)
         order_w1_plane(2)
-        hidden_matmul(WIDE, 1, 0)
-        hidden_matmul(WIDE, 1, 1)
-        hidden_matmul(WIDE, 1, 2)
-        hidden_matmul(WIDE, 1, 3)
-        group_w2(1, 0, True)
-        scale_hidden(WIDE, 0)
-        quantize_hidden(NARROW, 0)
+        scale_wide(0)
+        quantize_h(NARROW, 0)
+
+        hidden_matmuls(WIDE, 1)
+        group_w2(1, 0, on_scalar)
+        group_wide(0)
         order_w1_codes(3)
         order_w1_plane(3)
-        quantize_hidden(WIDE, 0)
-        hidden_matmul(WIDE, 2, 0)
-        hidden_matmul(WIDE, 2, 1)
-        hidden_matmul(WIDE, 2, 2)
-        hidden_matmul(WIDE, 2, 3)
-        gelu(WIDE, 1, 0)
-        gelu(WIDE, 1, 1)
-        gelu(WIDE, 1, 2)
-        gelu(WIDE, 1, 3)
-        group_w2(2, 1, False)
-        gelu(WIDE, 2, 0)
-        gelu(WIDE, 2, 1)
-        gelu(WIDE, 2, 2)
-        gelu(WIDE, 2, 3)
-        scale_hidden(WIDE, 1)
+        quantize_h(WIDE, 0)
+
+        hidden_matmuls(WIDE, 2)
+        gelu(WIDE, 1)
+        group_w2(2, 1, on_vector)
+        gelu(WIDE, 2)
+        scale_wide(1)
         quantize_w2(1, 0)
-        hidden_matmul(WIDE, 3, 0)
-        hidden_matmul(WIDE, 3, 1)
-        hidden_matmul(WIDE, 3, 2)
-        hidden_matmul(WIDE, 3, 3)
-        group_w2(2, 0, True)
-        scale_hidden(WIDE, 2)
-        quantize_hidden(WIDE, 1)
-        gelu(WIDE, 3, 0)
-        gelu(WIDE, 3, 1)
-        gelu(WIDE, 3, 2)
-        gelu(WIDE, 3, 3)
+        group_wide(1)
+
+        hidden_matmuls(WIDE, 3)
+        group_w2(2, 0, on_scalar)
+        scale_wide(2)
+        quantize_h(WIDE, 1)
+        group_wide(2)
+        gelu(WIDE, 3)
         quantize_w2(2, 0)
-        hidden_matmul(NARROW, 1, 0)
-        hidden_matmul(NARROW, 1, 1)
-        hidden_matmul(NARROW, 2, 0)
-        hidden_matmul(NARROW, 2, 1)
-        group_w2(3, 0, True)
-        scale_hidden(WIDE, 3)
-        quantize_hidden(WIDE, 2)
-        quantize_w2(3, 0)
-        quantize_hidden(WIDE, 3)
-        gelu(NARROW, 1, 0)
-        gelu(NARROW, 1, 1)
-        hidden_matmul(NARROW, 3, 0)
-        hidden_matmul(NARROW, 3, 1)
-        group_w2(0, 1, True)
-        bias_product()
-        group_w2(3, 1, False)
-        group_w2(1, 1, True)
-        gelu(NARROW, 2, 0)
-        gelu(NARROW, 2, 1)
-        project(WIDE, 0, 0)
-        project(WIDE, 0, 1)
-        project(WIDE, 0, 2)
-        project(WIDE, 0, 3)
+        quantize_h(WIDE, 2)
+
+        hidden_matmuls(NARROW, 1)
+        hidden_matmuls(NARROW, 2)
+        group_w2(3, 0, on_scalar)
+        scale_wide(3)
         quantize_w2(2, 1)
+        group_wide(3)
+        quantize_w2(3, 0)
+        quantize_h(WIDE, 3)
+
+        gelu(NARROW, 1)
+        hidden_matmuls(NARROW, 3)
+        group_w2(0, 1, on_scalar)
+        prepare_epilogue_constants()
+        group_w2(3, 1, on_vector)
+        group_w2(1, 1, on_vector)
+        gelu(NARROW, 2)
+
+        project(WIDE, 0)
         quantize_w2(0, 1)
         quantize_w2(3, 1)
         quantize_w2(1, 1)
-        gelu(NARROW, 3, 0)
-        gelu(NARROW, 3, 1)
-        affine(WIDE, 0, 0, True)
-        affine(WIDE, 0, 1, True)
-        affine(WIDE, 0, 2, True)
-        affine(WIDE, 0, 3, True)
-        project(WIDE, 1, 0)
-        project(WIDE, 1, 1)
-        project(WIDE, 1, 2)
-        project(WIDE, 1, 3)
-        scale_hidden(NARROW, 1)
-        scale_hidden(NARROW, 2)
-        quantize_hidden(NARROW, 1)
-        scale_hidden(NARROW, 3)
-        quantize_hidden(NARROW, 2)
-        quantize_hidden(NARROW, 3)
-        affine(WIDE, 1, 0, True)
-        affine(WIDE, 1, 1, True)
-        affine(WIDE, 1, 2, True)
-        affine(WIDE, 1, 3, True)
-        cap_bank = turn_caption_weight()
-        caption_column(cap_bank, True)
-        turn(0, 0)
-        turn(1, 0)
-        turn(2, 0)
-        turn(3, 0)
-        rows_out(0, 0, True)
-        rows_out(1, 0, True)
-        project(NARROW, 0, 0)
-        project(NARROW, 0, 1)
-        rows_out(2, 0, True)
-        rows_out(3, 0, True)
+        gelu(NARROW, 3)
+        affine(WIDE, 0)
+
+        project(WIDE, 1)
+        scale_narrow(1)
+        scale_narrow(2)
+        quantize_h(NARROW, 1)
+        scale_narrow(3)
+        quantize_h(NARROW, 2)
+        quantize_h(NARROW, 3)
+        affine(WIDE, 1)
+
+        place_caption_weight()
+        turn(WIDE_TILES, 0)
+        store_rows(WIDE_TILES, 0)
+        project(NARROW, 0)
         scale_y(WIDE, 0)
-        affine(NARROW, 0, 0, True)
-        affine(NARROW, 0, 1, True)
-        turn(0, 1)
-        turn(1, 1)
-        turn(2, 1)
-        turn(3, 1)
-        turn(4, 0)
-        turn(5, 0)
+        affine(NARROW, 0)
+
+        turn(WIDE_TILES, 1)
+        turn(NARROW_TILES, 0)
         scale_y(WIDE, 1)
-        rows_out(0, 1, True)
-        rows_out(1, 1, True)
-        rows_out(2, 1, True)
-        rows_out(3, 1, True)
-        project(NARROW, 1, 0)
-        project(NARROW, 1, 1)
+        store_rows(WIDE_TILES, 1)
+        store_rows(NARROW_TILES, 0)
+        project(NARROW, 1)
         quantize_y(WIDE, 0)
         scale_y(NARROW, 0)
         quantize_y(WIDE, 1)
-        affine(NARROW, 1, 0, True)
-        affine(NARROW, 1, 1, True)
+        affine(NARROW, 1)
         quantize_y(NARROW, 0)
-        rows_out(4, 0, True)
-        rows_out(5, 0, True)
-        turn(4, 1)
-        turn(5, 1)
+
+        turn(NARROW_TILES, 1)
         scale_y(NARROW, 1)
-        rows_out(4, 1, True)
-        rows_out(5, 1, True)
+        store_rows(NARROW_TILES, 1)
         quantize_y(NARROW, 1)
-        store_plane()
+        store_y_plane()

from contextlib import ExitStack

import concourse.mybir as mybir
from concourse.masks import make_identity

M, K, F, D = 768, 1536, 2048, 1024
FLOPS = 2 * M * K * F + 2 * M * F * D

F32 = mybir.dt.float32
BF16 = mybir.dt.bfloat16
I32 = mybir.dt.int32
U32 = mybir.dt.uint32
U8 = mybir.dt.uint8
FP8X4 = mybir.dt.float8_e4m3fn_x4
FP4X4 = mybir.dt.float4_e2m1fn_x4
ACT = mybir.ActivationFunctionType
MULT = mybir.AluOpType.mult

P = 128
SLOTS = 4
SPAN = P * SLOTS
RUN = 8
K_PASSES = K // SPAN
F_GROUPS = F // SPAN
D_HALVES = D // SPAN
BANKS = 8
BANK_COLUMNS = 512
QUADRANT = 32
SCALE_ROWS = 4

WIDE, NARROW = "wide", "narrow"
CHUNK = {WIDE: (0, BANK_COLUMNS), NARROW: (BANK_COLUMNS, M - BANK_COLUMNS)}
WIDE_TILES = range(0, BANK_COLUMNS // P)
NARROW_TILES = range(BANK_COLUMNS // P, M // P)

F32_BUFS, SCALED_BUFS, GROUPED_BUFS, W2_GROUPED_BUFS, ROW_BUFS = 4, 3, 4, 6, 6


def tile_caption_shared_embedding_h2_kernel(
    tc, x_words, x_scales, w1_words, w1_scales, hidden_scale, w2, b2, dim_weight, caption_weight, out_0, out_1, out_2
):
    nc = tc.nc
    with ExitStack() as ctx:
        keep = ctx.enter_context(tc.tile_pool(name="keep", bufs=1))
        work = ctx.enter_context(tc.tile_pool(name="work", bufs=1))
        psum = ctx.enter_context(tc.psum_pool(name="psum", bufs=1))
        ctx.enter_context(tc.manual_schedule())

        banks_used = []

        def next_bank(shape, dtype):
            count = len(banks_used)
            banks_used.append(count)
            return psum.tile(shape, dtype, name="bank_%d" % count, tag="bank%d" % (count % BANKS))

        def kept(name, shape, dtype):
            return keep.tile(shape, dtype, name=name, align_bytes=64)

        groups = range(F_GROUPS)
        halves = range(D_HALVES)
        x_codes = {c: kept("x_codes_" + c, [P, K_PASSES, CHUNK[c][1]], I32) for c in CHUNK}
        x_plane = kept("x_plane", [P, K_PASSES, M], U8)
        w1_raw = [kept("w1_raw%d" % g, [P, K_PASSES, SPAN // 2], I32) for g in groups]
        w1_plane_first = kept("w1_plane_first", [P, K_PASSES, SPAN], U8)
        w1_plane_rest = kept("w1_plane_rest", [P, K_PASSES, F - SPAN], U8)
        w1_codes = [kept("w1_codes%d" % g, [P, SLOTS, K_PASSES, 2 * P], U8) for g in groups]
        w1_plane = [kept("w1_plane%d" % g, [P, SLOTS, K_PASSES, P], U8) for g in groups]
        w2_raw = {(g, h): kept("w2_raw%d%d" % (g, h), [P, SLOTS, SPAN], BF16) for g in groups for h in halves}
        w2_codes = {(g, h): kept("w2_codes%d%d" % (g, h), [P, SPAN], U32) for g in groups for h in halves}
        w2_plane = {(g, h): kept("w2_plane%d%d" % (g, h), [P, SPAN], U8) for g in groups for h in halves}
        h_codes = {(c, g): kept("h_codes%s%d" % (c, g), [P, CHUNK[c][1]], U32) for c in CHUNK for g in groups}
        h_plane = {(c, g): kept("h_plane%s%d" % (c, g), [P, CHUNK[c][1]], U8) for c in CHUNK for g in groups}
        y_codes = {(c, h): kept("y_codes%s%d" % (c, h), [P, CHUNK[c][1]], U32) for c in CHUNK for h in halves}
        y_plane = kept("y_plane", [P, D_HALVES, M], U8)
        gain_raw = kept("gain_raw", [F_GROUPS, SPAN], BF16)
        gain_rows = kept("gain_rows", [P, SPAN], F32)
        gain = kept("gain", [P, F_GROUPS, SLOTS], F32)
        b2_col = kept("b2_col", [P, D_HALVES, SLOTS], BF16)
        dim_col = kept("dim_col", [P, D_HALVES, SLOTS], BF16)
        dim_f32 = kept("dim_f32", [P, D_HALVES, SLOTS], F32)
        bias = kept("bias", [P, D_HALVES, SLOTS], F32)
        cap_row = kept("cap_row", [P, M], BF16)
        cap_col = kept("cap_col", [P, M // P], F32)
        ident = kept("ident", [P, P], F32)
        ident_bf = kept("ident_bf", [P, P], BF16)

        def load_x(c):
            m0, width = CHUNK[c]
            src = x_words.rearrange("k p m t -> p k (m t)")[:, :, SLOTS * m0 : SLOTS * (m0 + width)]
            nc.sync.dma_start(out=x_codes[c][:], in_=src.bitcast(I32))

        def load_w1(g):
            src = w1_words.rearrange("k p n -> p k n")[:, :, 2 * SPAN * g : 2 * SPAN * (g + 1)]
            nc.sync.dma_start(out=w1_raw[g][:], in_=src.bitcast(I32))

        def load_plane(plane, scales):
            src = scales.rearrange("k q n -> q k n")
            for r in range(SCALE_ROWS):
                nc.sync.dma_start(out=plane[r:P:QUADRANT].bitcast(I32), in_=src[r : P // RUN : SCALE_ROWS].bitcast(I32))

        def load_w2(g, h):
            src = w2[SPAN * g : SPAN * (g + 1), SPAN * h : SPAN * (h + 1)]
            src = src.rearrange("(q t r) n -> t q r n", t=SLOTS, r=RUN)
            for t in range(SLOTS):
                nc.sync.dma_start(out=w2_raw[g, h][:, t, :], in_=src[t])

        nc.vector.memset(w1_plane_first[:].bitcast(I32), 0)
        nc.vector.memset(x_plane[:].bitcast(I32), 0)
        nc.vector.memset(ident[:], 0.0)
        make_identity(nc, ident[:], nomemset=True)
        nc.vector.memset(gain_rows[:], 0.0)
        nc.vector.memset(w1_plane_rest[:].bitcast(I32), 0)

        nc.sync.dma_start(out=gain_raw[:], in_=hidden_scale.rearrange("(g f) -> g f", f=SPAN))
        load_x(NARROW)
        load_w1(0)
        load_plane(w1_plane_first, w1_scales[:, :, :SPAN])
        load_plane(x_plane, x_scales)
        load_w2(0, 0)
        load_x(WIDE)
        load_w1(1)
        load_plane(w1_plane_rest, w1_scales[:, :, SPAN:])
        load_w1(2)
        load_w2(1, 0)
        load_w1(3)
        load_w2(2, 1)
        load_w2(2, 0)
        load_w2(3, 0)
        load_w2(0, 1)
        nc.sync.dma_start(out=b2_col[:], in_=b2.rearrange("(h p t) -> p h t", p=P, t=SLOTS))
        nc.sync.dma_start(out=dim_col[:], in_=dim_weight.rearrange("(h p t) -> p h t", p=P, t=SLOTS))
        load_w2(1, 1)
        load_w2(3, 1)
        nc.sync.dma_start(out=cap_row[:], in_=caption_weight.partition_broadcast(P))

        def place_gain():
            nc.scalar.copy(
                out=gain_rows[0:F_GROUPS, :].rearrange("g (t q r) -> g t q r", t=SLOTS, r=RUN),
                in_=gain_raw[:].rearrange("g (q t r) -> g t q r", t=SLOTS, r=RUN),
            )
            bank = next_bank([P, SLOTS, P], F32)
            for t in range(SLOTS):
                nc.tensor.transpose(bank[:, t, :], gain_rows[:, P * t : P * (t + 1)], ident[:])
            nc.scalar.copy(out=gain[:], in_=bank[:, :, 0:F_GROUPS].rearrange("p t g -> p g t"))

        def prepare_epilogue_constants():
            nc.vector.tensor_copy(out=ident_bf[:], in_=ident[:])
            nc.vector.tensor_copy(out=dim_f32[:], in_=dim_col[:])
            nc.vector.tensor_tensor(out=bias[:], in0=b2_col[:], in1=dim_col[:], op=MULT)

        def place_caption_weight():
            bank = next_bank([P, M // P, P], BF16)
            for i in range(M // P):
                nc.tensor.transpose(bank[:, i, :], cap_row[:, P * i : P * (i + 1)], ident_bf[:])
            nc.scalar.copy(out=cap_col[:], in_=bank[:, :, 0])

        def order_w1_codes(g):
            nc.vector.tensor_copy(
                out=w1_codes[g][:].bitcast(I32).rearrange("p t k (q w) -> p t (k q) w", w=RUN // 2),
                in_=w1_raw[g][:].rearrange("p k (q t w) -> p t (k q) w", t=SLOTS, w=RUN // 2),
            )

        def order_w1_plane(g):
            if g == 0:
                src = w1_plane_first[:].bitcast(I32)
            else:
                src = w1_plane_rest[:].bitcast(I32)[:, :, P * (g - 1) : P * g]
            nc.vector.tensor_copy(
                out=w1_plane[g][:].bitcast(I32).rearrange("p t k (q w) -> p t k q w", w=RUN // 4),
                in_=src.rearrange("p k (q t w) -> p t k q w", t=SLOTS, w=RUN // 4),
            )

        u_banks, gelu_of, scaled_of, h_grouped = {}, {}, {}, {}

        def hidden_matmuls(c, g):
            m0, width = CHUNK[c]

            def passes(out, t, first, count):
                for k in range(K_PASSES):
                    nc.tensor.matmul_mx(
                        out=out,
                        lhsT=w1_codes[g][:, t, k, :].bitcast(FP4X4),
                        lhsT_scale=w1_plane[g][:, t, k, :],
                        rhs=x_codes[c][:, k, first : first + count].bitcast(FP8X4),
                        rhs_scale=x_plane[:, k, m0 + first : m0 + first + count],
                        start=(k == 0),
                        stop=(k == K_PASSES - 1),
                    )

            u_banks[c, g] = []
            if c == WIDE:
                for t in range(SLOTS):
                    bank = next_bank([P, width], F32)
                    passes(bank[:], t, 0, width)
                    u_banks[c, g].append(bank)
            else:
                for first in range(0, width, P):
                    bank = next_bank([P, SLOTS, P], F32)
                    for t in range(SLOTS):
                        passes(bank[:, t, :], t, first, P)
                    u_banks[c, g].append(bank)

        def gelu(c, g):
            width = CHUNK[c][1]
            shape = [P, SLOTS, width] if c == WIDE else [P, width, SLOTS]
            values = work.tile(shape, F32, name="gelu_%s%d" % (c, g), tag="f32", bufs=F32_BUFS)
            for i, bank in enumerate(u_banks[c, g]):
                if c == WIDE:
                    out, src = values[:, i, :], bank[:]
                else:
                    out, src = values[:, P * i : P * (i + 1), :], bank[:].rearrange("p t m -> p m t")
                nc.scalar.activation(out=out, in_=src, func=ACT.Gelu_apprx_tanh)
            gelu_of[c, g] = values

        def grouped_tile(name, width):
            return work.tile([P, width, SLOTS], BF16, name=name, tag="grouped", bufs=GROUPED_BUFS, align_bytes=64)

        def scale_narrow(g):
            width = CHUNK[NARROW][1]
            grouped = grouped_tile("h_narrow%d" % g, width)
            factor = gain[:, g, :].unsqueeze(1).broadcast_to([P, width, SLOTS])
            nc.vector.tensor_tensor(out=grouped[:], in0=gelu_of[NARROW, g][:], in1=factor, op=MULT)
            h_grouped[NARROW, g] = grouped

        def scale_wide(g):
            scaled = work.tile([P, SLOTS, CHUNK[WIDE][1]], BF16, name="scaled%d" % g, tag="scaled", bufs=SCALED_BUFS)
            for t in range(SLOTS):
                nc.vector.tensor_scalar(
                    out=scaled[:, t, :], in0=gelu_of[WIDE, g][:, t, :], scalar1=gain[:, g, t : t + 1], scalar2=None, op0=MULT
                )
            scaled_of[g] = scaled

        def group_wide(g):
            grouped = grouped_tile("h_wide%d" % g, CHUNK[WIDE][1])
            nc.vector.tensor_copy(out=grouped[:], in_=scaled_of[g][:].rearrange("p t m -> p m t"))
            h_grouped[WIDE, g] = grouped

        def quantize(codes, plane, grouped):
            nc.vector.quantize_mx(out=codes.bitcast(FP8X4), scales=plane, in_=grouped[:].rearrange("p n t -> p (n t)"))

        def quantize_h(c, g):
            quantize(h_codes[c, g][:], h_plane[c, g][:], h_grouped[c, g])

        w2_grouped = {}

        def group_w2(g, h, copy):
            grouped = work.tile(
                [P, SPAN, SLOTS], BF16, name="w2_grouped%d%d" % (g, h), tag="w2_grouped", bufs=W2_GROUPED_BUFS, align_bytes=64
            )
            copy(
                out=grouped[:].rearrange("p (t n) j -> p n j t", t=SLOTS),
                in_=w2_raw[g, h][:].rearrange("p j (n t) -> p n j t", t=SLOTS),
            )
            w2_grouped[g, h] = grouped

        def quantize_w2(g, h):
            quantize(w2_codes[g, h][:], w2_plane[g, h][:], w2_grouped[g, h])

        z_banks, affine_of, turned, y_grouped = {}, {}, {}, {}

        def project(c, h):
            width = CHUNK[c][1]
            per_bank = BANK_COLUMNS // width
            z_banks[c, h] = []
            for t in range(SLOTS):
                if t % per_bank == 0:
                    bank = next_bank([P, per_bank, width], F32)
                out = bank[:, t % per_bank, :]
                for g in groups:
                    nc.tensor.matmul_mx(
                        out=out,
                        lhsT=w2_codes[g, h][:, P * t : P * (t + 1)].bitcast(FP8X4),
                        lhsT_scale=w2_plane[g, h][:, P * t : P * (t + 1)],
                        rhs=h_codes[c, g][:].bitcast(FP8X4),
                        rhs_scale=h_plane[c, g][:],
                        start=(g == 0),
                        stop=(g == F_GROUPS - 1),
                    )
                z_banks[c, h].append(out)

        def affine(c, h):
            values = work.tile([P, SLOTS, CHUNK[c][1]], F32, name="affine_%s%d" % (c, h), tag="f32", bufs=F32_BUFS)
            for t in range(SLOTS):
                nc.scalar.activation(
                    out=values[:, t, :],
                    in_=z_banks[c, h][t],
                    func=ACT.Identity,
                    scale=dim_f32[:, h, t : t + 1],
                    bias=bias[:, h, t : t + 1],
                )
            affine_of[c, h] = values

        def turn(tiles, h):
            for i in tiles:
                c = WIDE if i in WIDE_TILES else NARROW
                first = P * i - CHUNK[c][0]
                bank = next_bank([P, SLOTS, P], F32)
                for t in range(SLOTS):
                    nc.tensor.transpose(bank[:, t, :], affine_of[c, h][:, t, first : first + P], ident[:])
                turned[i, h] = bank

        def store_rows(tiles, h):
            for i in tiles:
                rows = work.tile([P, P, SLOTS], F32, name="rows_%d%d" % (i, h), tag="rows", bufs=ROW_BUFS)
                nc.scalar.activation(
                    out=rows[:], in_=turned[i, h][:].rearrange("m t p -> m p t"), func=ACT.Copy, scale=cap_col[:, i : i + 1]
                )
                nc.sync.dma_start(
                    out=out_0[P * i : P * (i + 1), SPAN * h : SPAN * (h + 1)], in_=rows[:].rearrange("m p t -> m (p t)")
                )

        def scale_y(c, h):
            m0, width = CHUNK[c]
            grouped = grouped_tile("y_%s%d" % (c, h), width)
            nc.vector.tensor_tensor(
                out=grouped[:],
                in0=affine_of[c, h][:].rearrange("p t m -> p m t"),
                in1=cap_row[:, m0 : m0 + width].unsqueeze(2).broadcast_to([P, width, SLOTS]),
                op=MULT,
            )
            y_grouped[c, h] = grouped

        def quantize_y(c, h):
            m0, width = CHUNK[c]
            quantize(y_codes[c, h][:], y_plane[:, h, m0 : m0 + width], y_grouped[c, h])
            dst = out_1[h].rearrange("p m t -> p (m t)")[:, SLOTS * m0 : SLOTS * (m0 + width)]
            nc.sync.dma_start(out=dst.bitcast(I32), in_=y_codes[c, h][:].bitcast(I32))

        def store_y_plane():
            dst = out_2.rearrange("h q m -> q h m")
            for r in range(SCALE_ROWS):
                nc.sync.dma_start(out=dst[r : P // RUN : SCALE_ROWS].bitcast(I32), in_=y_plane[r:P:QUADRANT].bitcast(I32))

        on_vector, on_scalar = nc.vector.tensor_copy, nc.scalar.copy

        place_gain()
        order_w1_codes(0)
        order_w1_plane(0)
        hidden_matmuls(NARROW, 0)
        gelu(NARROW, 0)
        group_w2(0, 0, on_vector)

        hidden_matmuls(WIDE, 0)
        gelu(WIDE, 0)
        order_w1_codes(1)
        quantize_w2(0, 0)
        order_w1_plane(1)
        scale_narrow(0)
        order_w1_codes(2)
        order_w1_plane(2)
        scale_wide(0)
        quantize_h(NARROW, 0)

        hidden_matmuls(WIDE, 1)
        group_w2(1, 0, on_scalar)
        group_wide(0)
        order_w1_codes(3)
        order_w1_plane(3)
        quantize_h(WIDE, 0)

        hidden_matmuls(WIDE, 2)
        gelu(WIDE, 1)
        group_w2(2, 1, on_vector)
        gelu(WIDE, 2)
        scale_wide(1)
        quantize_w2(1, 0)
        group_wide(1)

        hidden_matmuls(WIDE, 3)
        group_w2(2, 0, on_scalar)
        scale_wide(2)
        quantize_h(WIDE, 1)
        group_wide(2)
        gelu(WIDE, 3)
        quantize_w2(2, 0)
        quantize_h(WIDE, 2)

        hidden_matmuls(NARROW, 1)
        hidden_matmuls(NARROW, 2)
        group_w2(3, 0, on_scalar)
        scale_wide(3)
        quantize_w2(2, 1)
        group_wide(3)
        quantize_w2(3, 0)
        quantize_h(WIDE, 3)

        gelu(NARROW, 1)
        hidden_matmuls(NARROW, 3)
        group_w2(0, 1, on_scalar)
        prepare_epilogue_constants()
        group_w2(3, 1, on_vector)
        group_w2(1, 1, on_vector)
        gelu(NARROW, 2)

        project(WIDE, 0)
        quantize_w2(0, 1)
        quantize_w2(3, 1)
        quantize_w2(1, 1)
        gelu(NARROW, 3)
        affine(WIDE, 0)

        project(WIDE, 1)
        scale_narrow(1)
        scale_narrow(2)
        quantize_h(NARROW, 1)
        scale_narrow(3)
        quantize_h(NARROW, 2)
        quantize_h(NARROW, 3)
        affine(WIDE, 1)

        place_caption_weight()
        turn(WIDE_TILES, 0)
        store_rows(WIDE_TILES, 0)
        project(NARROW, 0)
        scale_y(WIDE, 0)
        affine(NARROW, 0)

        turn(WIDE_TILES, 1)
        turn(NARROW_TILES, 0)
        scale_y(WIDE, 1)
        store_rows(WIDE_TILES, 1)
        store_rows(NARROW_TILES, 0)
        project(NARROW, 1)
        quantize_y(WIDE, 0)
        scale_y(NARROW, 0)
        quantize_y(WIDE, 1)
        affine(NARROW, 1)
        quantize_y(NARROW, 0)

        turn(NARROW_TILES, 1)
        scale_y(NARROW, 1)
        store_rows(NARROW_TILES, 1)
        quantize_y(NARROW, 1)
        store_y_plane()
